import numpy as np
import ml_dtypes


def mxq(x, axis, fmt="e4m3"):
    dtype, down = {"e4m3": (ml_dtypes.float8_e4m3fn, 7), "e5m2": (ml_dtypes.float8_e5m2, 14)}[fmt]
    v = np.moveaxis(np.asarray(x, np.float32).astype(ml_dtypes.bfloat16).astype(np.float64), axis, -1)
    blocks = v.reshape(v.shape[:-1] + (-1, 32))
    amax = np.abs(blocks).max(-1, keepdims=True)
    byte = np.maximum(np.where(amax > 0, np.frexp(amax)[1] - 1 + 127, 0) - down, 1)
    scale = np.exp2(byte - 127.0)
    codes = (blocks / scale).astype(np.float32).astype(dtype).astype(np.float64)
    return np.moveaxis((codes * scale).reshape(v.shape), -1, axis)


WIDE = False


def mx_kscale(k):
    if not WIDE:
        return np.ones(k)
    levels = np.array([10, -10, 5, -5, 0])
    if k % 512:
        return np.exp2(np.random.permutation(np.resize(levels, k // 32))).repeat(32)
    a = np.empty((k // 512, 16))
    for p in range(k // 512):
        a[p, :8] = np.random.permutation(np.resize(levels, 8))
        for g in range(8):
            far = levels[np.abs(levels - a[p, g]) >= 10]
            a[p, g + 8] = far[np.random.randint(len(far))]
    return np.exp2(a.ravel()).repeat(32)


def f64(x):
    return np.asarray(x).astype(np.float64)


def striped(idx):
    return np.tile(np.asarray(idx).reshape(-1, 16).T, (8, 1)).astype(np.uint16)


def unstriped(offs):
    return offs[:16].T.reshape(-1).astype(np.int64)


E2M1 = np.array([0.0, 0.5, 1.0, 1.5, 2.0, 3.0, 4.0, 6.0, -0.0, -0.5, -1.0, -1.5, -2.0, -3.0, -4.0, -6.0])


def pack_weight(w, fmt):
    k, n = w.shape
    w = f64(np.asarray(w, np.float32).astype(ml_dtypes.bfloat16)).reshape(k // 32, 32, n)
    amax = np.abs(w).max(1)
    if fmt == "e4m3":
        byte = np.frexp(amax)[1] - 1 + 127 - 7
    else:
        mant, ex = np.frexp(amax / 6.0)
        byte = np.where(mant > 0.5, ex, ex - 1) + 127
    byte = np.clip(np.where(amax > 0, byte, 1), 1, 254)
    scaled = (w * np.exp2(127.0 - byte)[:, None, :]).reshape(k, n).astype(np.float32)
    by_word = np.ascontiguousarray(scaled.reshape(k // 512, 128, 4, n).transpose(0, 1, 3, 2))
    if fmt == "e4m3":
        words = by_word.astype(ml_dtypes.float8_e4m3fn).view(np.uint8)
    else:
        c = by_word.astype(ml_dtypes.float4_e2m1fn).view(np.uint8) & 0xF
        words = (c[..., 0::2] | (c[..., 1::2] << 4)).reshape(k // 512, 128, 2 * n)
    return np.ascontiguousarray(words), np.ascontiguousarray(byte.astype(np.uint8).reshape(k // 512, 16, n))


def unpack_weight(words, scales, fmt):
    g, _, n = scales.shape
    words = np.ascontiguousarray(words).reshape(g, 128, n, -1)
    if fmt == "e4m3":
        vals = words.view(ml_dtypes.float8_e4m3fn).astype(np.float64)
    else:
        nib = np.empty((g, 128, n, 4), np.uint8)
        nib[..., 0::2] = words & 0xF
        nib[..., 1::2] = words >> 4
        vals = E2M1[nib]
    vals = vals * np.repeat(np.exp2(scales.astype(np.float64) - 127.0), 8, axis=1)[..., None]
    return vals.transpose(0, 1, 3, 2).reshape(g * 512, n)


def sigmoid(v):
    return 1.0 / (1.0 + np.exp(-v))


def bf(x):
    return np.asarray(x, np.float32).astype(ml_dtypes.bfloat16)


def planes(Y):
    r, m = Y.shape
    b = f64(bf(Y)).reshape(r // 32, 32, m)
    amax = np.abs(b).max(1)
    byte = np.clip(np.where(amax > 0, np.frexp(amax)[1] - 1 + 127 - 7, 1), 1, 254)
    codes = (b * np.exp2(127.0 - byte)[:, None, :]).reshape(r, m).astype(np.float32).astype(ml_dtypes.float8_e4m3fn).view(np.uint8)
    words = codes.reshape(r // 512, 128, 4, m).transpose(0, 1, 3, 2)
    return np.ascontiguousarray(words), np.ascontiguousarray(byte.astype(np.uint8).reshape(r // 512, 16, m))


B, N, T, D, NQ = 1, 512, 2048, 1024, 512


def setup_inputs():
    n = np.random.standard_normal
    pages = np.random.permutation(T // 32)[:B * N // 32]
    idx = (pages[:, None] * 32 + np.arange(32)[None, :]).reshape(-1)
    s = mx_kscale(D)[:, None]
    kp = pack_weight(n((D, T)) / s, "e2m1")
    return {
        "qT": (n((B, D, NQ)) * s * (1.00 / np.sqrt(D))).astype(np.float32),
        "k_words": np.ascontiguousarray(kp[0].reshape(1, 2, 128, T, 2).transpose(0, 2, 3, 1, 4)).reshape(1, 128, T, 4),
        "k_scales": kp[1],
        "ts": np.tile(np.random.uniform(0.5, 2.0, 2048), (128, 1)).astype(np.float32),
        "kb": np.tile(n(2048), (128, 1)).astype(np.float32),
        "offs": striped(idx),
    }


def reference(qT, k_words, k_scales, ts, kb, offs):
    idx = unstriped(offs)
    pick = lambda x, which: x[:, which].reshape(x.shape[0], B, -1).transpose(1, 0, 2)
    k = unpack_weight(k_words.reshape(1, 128, T, 2, 2).transpose(0, 3, 1, 2, 4).reshape(2, 128, 2 * T), k_scales, "e2m1")
    kg = pick(k, idx)
    qq = mxq(f64(qT), 1, "e4m3")
    a = kg.transpose(0, 2, 1) @ qq
    y = sigmoid(a * pick(f64(ts), idx)[:, :1, :].transpose(0, 2, 1) + pick(f64(kb), idx)[:, :1, :].transpose(0, 2, 1))
    Y = y[0]
    words, scales = planes(Y)
    return Y, words, scales

@@ -1,0 +1,176 @@
+from contextlib import ExitStack
+
+import concourse.mybir as mybir
+from concourse.masks import make_identity
+
+N, T, D, NQ = 512, 2048, 1024, 512
+FLOPS = 2 * N * D * NQ
+BYTES = 4 * D * NQ + 128 * T * 4 + 32 * T + 2 * 4 * T + 128 * 32 * 2 + 4 * N * NQ + N * NQ + 16 * NQ
+
+F32 = mybir.dt.float32
+BF16 = mybir.dt.bfloat16
+I32 = mybir.dt.int32
+U32 = mybir.dt.uint32
+U16 = mybir.dt.uint16
+U8 = mybir.dt.uint8
+FP8X4 = mybir.dt.float8_e4m3fn_x4
+FP4X4 = mybir.dt.float4_e2m1fn_x4
+SIGMOID = mybir.ActivationFunctionType.Sigmoid
+
+P = 128
+PACK = 4
+PASSES = D // (P * PACK)
+HALF = NQ // 2
+NMM = 128
+LIVE = P - 1
+
+
+def interleave(engine_copy, dst, src):
+    engine_copy(dst.rearrange("p (c i) t -> p c t i", i=4), src.rearrange("p t (c i) -> p c t i", i=4))
+
+
+def tile_attend_plw_tskb_kernel(tc, qT, k_words, k_scales, ts, kb, offs, out_0, out_1, out_2):
+    nc = tc.nc
+    with ExitStack() as ctx:
+        keep = ctx.enter_context(tc.tile_pool(name="keep", bufs=1))
+        psum = ctx.enter_context(tc.psum_pool(name="psum", bufs=1))
+
+        offsets = keep.tile([P, N // 16], U16, name="offsets")
+        nc.sync.dma_start(offsets[:], offs)
+
+        scale_pool = keep.tile([P, T], U8, name="scale_pool", align_bytes=64)
+        nc.gpsimd.memset(scale_pool[:].bitcast(I32), 0)
+        ts_pool = keep.tile([P, T], F32, name="ts_pool")
+        kb_pool = keep.tile([P, T], F32, name="kb_pool")
+        nc.sync.dma_start(ts_pool[LIVE:P, :], ts[0:1, :])
+        nc.sync.dma_start(kb_pool[LIVE:P, :], kb[0:1, :])
+        for quad in range(4):
+            nc.sync.dma_start(
+                scale_pool[32 * quad : 32 * quad + 8, :].bitcast(I32),
+                k_scales[:, 4 * quad : 4 * quad + 4, :].bitcast(I32),
+            )
+        nc.vector.memset(ts_pool[0:LIVE, :], 0.0)
+
+        warm = keep.tile([P, 8], F32, name="warm")
+        warm_out = keep.tile([P, 8], F32, name="warm_out")
+        nc.gpsimd.memset(warm[:], 0.0)
+        nc.scalar.activation(warm_out[:], warm[:], SIGMOID)
+        k_scale = [keep.tile([P, N], U8, name="k_scale%d" % o, align_bytes=64) for o in range(PASSES)]
+        nc.gpsimd.memset(k_scale[1][:].bitcast(I32), 0)
+        ident = keep.tile([P, P], F32, name="ident")
+        make_identity(nc, ident[:])
+        nc.gpsimd.memset(kb_pool[0:LIVE, :], 0.0)
+
+        q_raw = {}
+
+        def load_q(h, o):
+            raw = keep.tile([P, PACK, HALF], F32, name="q_raw%d%d" % (h, o))
+            rows = qT[0, 512 * o : 512 * (o + 1), HALF * h : HALF * (h + 1)]
+            nc.sync.dma_start(raw[:], rows.rearrange("(p j) w -> p j w", j=PACK))
+            q_raw[(h, o)] = raw
+
+        word_pool = keep.tile([P, T], I32, name="word_pool", align_bytes=64)
+        nc.sync.dma_start(word_pool[:], k_words[0].rearrange("p t b -> p (t b)").bitcast(I32))
+        load_q(0, 0)
+        load_q(0, 1)
+        load_q(1, 0)
+        load_q(1, 1)
+
+        scale_picked = keep.tile([P, N], U8, name="scale_picked", align_bytes=64)
+        nc.vector.tensor_copy(scale_picked[:], scale_pool[:].indirect(offsets[:]))
+        nc.vector.tensor_copy(
+            k_scale[0][:].rearrange("p (r s) -> p r s", r=PACK),
+            scale_picked[:].rearrange("p (s r) -> p r s", r=PACK),
+        )
+        nc.scalar.dma_start(k_scale[1][0:112, :].bitcast(I32), k_scale[0][4:116, :].bitcast(I32))
+
+        def columns(pool_tile, name, bank):
+            picked = keep.tile([P, N], F32, name=name + "_picked")
+            nc.vector.tensor_copy(picked[:], pool_tile[:].indirect(offsets[:]))
+            turned = psum.tile([P, PACK, P], F32, name=name + "_turned", tag=bank)
+            for r in range(PACK):
+                nc.tensor.transpose(turned[:, r, :], picked[:, r:N:PACK], ident[:])
+            col = keep.tile([P, PACK], F32, name=name + "_col")
+            return turned, col
+
+        ts_turned, ts_col = columns(ts_pool, "ts", "bank6")
+        kb_turned, kb_col = columns(kb_pool, "kb", "bank7")
+
+        word_picked = keep.tile([P, N], U32, name="word_picked", align_bytes=64)
+        nc.vector.tensor_copy(
+            word_picked[:].rearrange("p (r s) -> p s r", r=PACK),
+            word_pool[:].bitcast(U32).indirect(offsets[:]),
+        )
+        k_code = keep.tile([P, PASSES, 2 * N], U8, name="k_code", align_bytes=64)
+        nc.vector.tensor_copy(
+            k_code[:].bitcast(U16),
+            word_picked[:].bitcast(U16).rearrange("p (c o) -> p o c", o=PASSES),
+        )
+
+        nc.vector.tensor_copy(ts_col[:], ts_turned[:, :, LIVE])
+        nc.vector.tensor_copy(kb_col[:], kb_turned[:, :, LIVE])
+
+        q_code = {}
+        q_scale = {}
+
+        def cast_q(h, o, engine_copy):
+            grouped = keep.tile([P, HALF, PACK], BF16, name="q_grouped%d%d" % (h, o), align_bytes=64)
+            interleave(engine_copy, grouped[:], q_raw[(h, o)][:])
+            return grouped
+
+        def quantize_q(h, o, grouped):
+            q_code[(h, o)] = keep.tile([P, HALF], U32, name="q_code%d%d" % (h, o), align_bytes=64)
+            q_scale[(h, o)] = keep.tile([P, HALF], U8, name="q_scale%d%d" % (h, o), align_bytes=64)
+            nc.vector.quantize_mx(
+                out=q_code[(h, o)][:].bitcast(FP8X4),
+                scales=q_scale[(h, o)][:],
+                in_=grouped[:].rearrange("p w j -> p (w j)"),
+            )
+
+        def one_pass(acc, h, r, a, o):
+            cols = slice(NMM * a, NMM * (a + 1))
+            nc.tensor.matmul_mx(
+                out=acc[:, cols],
+                lhsT=k_code[:, o, 2 * P * r : 2 * P * (r + 1)].bitcast(FP4X4),
+                lhsT_scale=k_scale[o][:, P * r : P * (r + 1)],
+                rhs=q_code[(h, o)][:, cols].bitcast(FP8X4),
+                rhs_scale=q_scale[(h, o)][:, cols],
+                start=(o == 0),
+                stop=(o == PASSES - 1),
+            )
+
+        y_code = keep.tile([P, NQ], U32, name="y_code", align_bytes=64)
+        y_scale = keep.tile([P, NQ], U8, name="y_scale", align_bytes=64)
+        y_rows = out_0.rearrange("(p r) q -> p r q", r=PACK)
+        y_words = out_1[0].rearrange("p q u -> p (q u)").bitcast(I32)
+
+        for h in range(2):
+            for o in range(PASSES):
+                last = (h, o) == (1, PASSES - 1)
+                quantize_q(h, o, cast_q(h, o, nc.vector.tensor_copy if last else nc.scalar.copy))
+
+        for h in range(2):
+            cols = slice(HALF * h, HALF * (h + 1))
+            acc = [psum.tile([P, HALF], F32, name="acc%d%d" % (h, r), tag="bank%d" % (4 * h + r)) for r in range(PACK)]
+            y = keep.tile([P, PACK, HALF], F32, name="y%d" % h)
+            for r in range(PACK):
+                one_pass(acc[r], h, r, 0, 0)
+            for r in range(PACK):
+                one_pass(acc[r], h, r, 0, 1)
+                one_pass(acc[r], h, r, 1, 0)
+                one_pass(acc[r], h, r, 1, 1)
+                nc.scalar.activation(y[:, r, :], acc[r][:], SIGMOID, bias=kb_col[:, r : r + 1], scale=ts_col[:, r : r + 1])
+            nc.sync.dma_start(y_rows[:, :, cols], y[:])
+            y_grouped = keep.tile([P, HALF, PACK], BF16, name="y_grouped%d" % h, align_bytes=64)
+            interleave(nc.vector.tensor_copy, y_grouped[:], y[:])
+            nc.vector.quantize_mx(
+                out=y_code[:, cols].bitcast(FP8X4),
+                scales=y_scale[:, cols],
+                in_=y_grouped[:].rearrange("p w j -> p (w j)"),
+            )
+            nc.sync.dma_start(y_words[:, cols], y_code[:, cols].bitcast(I32))
+        for quad in range(4):
+            nc.scalar.dma_start(
+                out_2[0, 4 * quad : 4 * quad + 4, :].bitcast(I32),
+                y_scale[32 * quad : 32 * quad + 4, :].bitcast(I32),
+            )

@@ -23,6 +23,7 @@ PASSES = D // (P * PACK)
 HALF = NQ // 2
 NMM = 128
 LIVE = P - 1
+SROW = 96
 
 
 def interleave(engine_copy, dst, src):
@@ -39,102 +40,115 @@ def tile_attend_plw_tskb_kernel(tc, qT, k_words, k_scales, ts, kb, offs, out_0, 
         nc.sync.dma_start(offsets[:], offs)
 
         scale_pool = keep.tile([P, T], U8, name="scale_pool", align_bytes=64)
-        nc.gpsimd.memset(scale_pool[:].bitcast(I32), 0)
-        ts_pool = keep.tile([P, T], F32, name="ts_pool")
+        ts_pool = keep.tile([P, T + 1], F32, name="ts_pool")
         kb_pool = keep.tile([P, T], F32, name="kb_pool")
-        nc.sync.dma_start(ts_pool[LIVE:P, :], ts[0:1, :])
+        nc.sync.dma_start(
+            scale_pool[SROW:P, :].bitcast(I32),
+            k_scales.rearrange("o f t -> f o t").bitcast(I32),
+        )
+        nc.sync.dma_start(ts_pool[LIVE:P, 0:T], ts[0:1, :])
         nc.sync.dma_start(kb_pool[LIVE:P, :], kb[0:1, :])
-        for quad in range(4):
-            nc.sync.dma_start(
-                scale_pool[32 * quad : 32 * quad + 8, :].bitcast(I32),
-                k_scales[:, 4 * quad : 4 * quad + 4, :].bitcast(I32),
-            )
+
+        word_pool = keep.tile([P, T], I32, name="word_pool", align_bytes=64)
+        nc.sync.dma_start(word_pool[:], k_words[0].rearrange("p t b -> p (t b)").bitcast(I32))
+
+        q_raw = {}
+
+        def load_q(h, o):
+            raw = keep.tile([P, PACK, HALF], F32, name="q_raw%d%d" % (h, o), tag="raw%d%d" % (h, o), align_bytes=64)
+            rows = qT[0, 512 * o : 512 * (o + 1), HALF * h : HALF * (h + 1)]
+            nc.sync.dma_start(raw[:], rows.rearrange("(p j) w -> p j w", j=PACK))
+            q_raw[(h, o)] = raw
+
+        load_q(0, 0)
+        load_q(0, 1)
+        load_q(1, 0)
+
+        k_scale = keep.tile([P, PASSES, N], U8, name="k_scale", align_bytes=64)
+        nc.gpsimd.memset(scale_pool[0:SROW, :].bitcast(I32), 0)
         nc.vector.memset(ts_pool[0:LIVE, :], 0.0)
 
         warm = keep.tile([P, 8], F32, name="warm")
         warm_out = keep.tile([P, 8], F32, name="warm_out")
         nc.gpsimd.memset(warm[:], 0.0)
         nc.scalar.activation(warm_out[:], warm[:], SIGMOID)
-        k_scale = [keep.tile([P, N], U8, name="k_scale%d" % o, align_bytes=64) for o in range(PASSES)]
-        nc.gpsimd.memset(k_scale[1][:].bitcast(I32), 0)
+        nc.gpsimd.memset(kb_pool[0:LIVE, :], 0.0)
         ident = keep.tile([P, P], F32, name="ident")
         make_identity(nc, ident[:])
-        nc.gpsimd.memset(kb_pool[0:LIVE, :], 0.0)
+        nc.gpsimd.memset(k_scale[:].rearrange("p o n -> p (o n)").bitcast(I32), 0)
 
-        q_raw = {}
-
-        def load_q(h, o):
-            raw = keep.tile([P, PACK, HALF], F32, name="q_raw%d%d" % (h, o))
-            rows = qT[0, 512 * o : 512 * (o + 1), HALF * h : HALF * (h + 1)]
-            nc.sync.dma_start(raw[:], rows.rearrange("(p j) w -> p j w", j=PACK))
-            q_raw[(h, o)] = raw
-
-        word_pool = keep.tile([P, T], I32, name="word_pool", align_bytes=64)
-        nc.sync.dma_start(word_pool[:], k_words[0].rearrange("p t b -> p (t b)").bitcast(I32))
-        load_q(0, 0)
-        load_q(0, 1)
-        load_q(1, 0)
-        load_q(1, 1)
-
-        scale_picked = keep.tile([P, N], U8, name="scale_picked", align_bytes=64)
+        scale_picked = keep.tile([P, N], U8, name="scale_picked", tag="raw11", align_bytes=64)
         nc.vector.tensor_copy(scale_picked[:], scale_pool[:].indirect(offsets[:]))
+
+        def turned(pool_tile, name, bank):
+            picked = keep.tile([P, N], F32, name=name + "_picked")
+            nc.vector.tensor_copy(picked[:], pool_tile[:, 0:T].indirect(offsets[:]))
+            out = psum.tile([P, PACK, P], F32, name=name + "_turned", tag=bank)
+            for r in range(PACK):
+                nc.tensor.transpose(out[:, r, :], picked[:, r:N:PACK], ident[:])
+            return out
+
+        ts_turned = turned(ts_pool, "ts", "bank6")
+
+        scale_dealt = keep.tile([P, N], U8, name="scale_dealt", align_bytes=64)
         nc.vector.tensor_copy(
-            k_scale[0][:].rearrange("p (r s) -> p r s", r=PACK),
+            scale_dealt[:].rearrange("p (r s) -> p r s", r=PACK),
             scale_picked[:].rearrange("p (s r) -> p r s", r=PACK),
         )
-        nc.scalar.dma_start(k_scale[1][0:112, :].bitcast(I32), k_scale[0][4:116, :].bitcast(I32))
+        for quad in range(4):
+            nc.sync.dma_start(
+                k_scale[32 * quad : 32 * quad + 4, :, :].bitcast(I32),
+                scale_dealt[SROW + 8 * quad : SROW + 8 * quad + 8, :].bitcast(I32),
+            )
 
-        def columns(pool_tile, name, bank):
-            picked = keep.tile([P, N], F32, name=name + "_picked")
-            nc.vector.tensor_copy(picked[:], pool_tile[:].indirect(offsets[:]))
-            turned = psum.tile([P, PACK, P], F32, name=name + "_turned", tag=bank)
-            for r in range(PACK):
-                nc.tensor.transpose(turned[:, r, :], picked[:, r:N:PACK], ident[:])
-            col = keep.tile([P, PACK], F32, name=name + "_col")
-            return turned, col
+        load_q(1, 1)
 
-        ts_turned, ts_col = columns(ts_pool, "ts", "bank6")
-        kb_turned, kb_col = columns(kb_pool, "kb", "bank7")
+        kb_turned = turned(kb_pool, "kb", "bank7")
 
         word_picked = keep.tile([P, N], U32, name="word_picked", align_bytes=64)
-        nc.vector.tensor_copy(
-            word_picked[:].rearrange("p (r s) -> p s r", r=PACK),
-            word_pool[:].bitcast(U32).indirect(offsets[:]),
-        )
+        nc.vector.tensor_copy(word_picked[:], word_pool[:].bitcast(U32).indirect(offsets[:]))
         k_code = keep.tile([P, PASSES, 2 * N], U8, name="k_code", align_bytes=64)
         nc.vector.tensor_copy(
-            k_code[:].bitcast(U16),
-            word_picked[:].bitcast(U16).rearrange("p (c o) -> p o c", o=PASSES),
+            k_code[:].bitcast(U16).rearrange("p o (r s) -> p o s r", r=PACK),
+            word_picked[:].bitcast(U16).rearrange("p (s r o) -> p o s r", r=PACK, o=PASSES),
         )
 
-        nc.vector.tensor_copy(ts_col[:], ts_turned[:, :, LIVE])
-        nc.vector.tensor_copy(kb_col[:], kb_turned[:, :, LIVE])
+        q_code = [keep.tile([P, NQ], U32, name="q_code%d" % o, align_bytes=64) for o in range(PASSES)]
+        q_scale = [keep.tile([P, NQ], U8, name="q_scale%d" % o, align_bytes=64) for o in range(PASSES)]
 
-        q_code = {}
-        q_scale = {}
-
-        def cast_q(h, o, engine_copy):
-            grouped = keep.tile([P, HALF, PACK], BF16, name="q_grouped%d%d" % (h, o), align_bytes=64)
-            interleave(engine_copy, grouped[:], q_raw[(h, o)][:])
+        def cast_q(o, c0, width, engine_copy, tag):
+            h, first = divmod(c0, HALF)
+            grouped = keep.tile([P, width, PACK], BF16, name="q_grouped%d_%d" % (o, c0), tag=tag, align_bytes=64)
+            interleave(engine_copy, grouped[:], q_raw[(h, o)][:, :, first : first + width])
             return grouped
 
-        def quantize_q(h, o, grouped):
-            q_code[(h, o)] = keep.tile([P, HALF], U32, name="q_code%d%d" % (h, o), align_bytes=64)
-            q_scale[(h, o)] = keep.tile([P, HALF], U8, name="q_scale%d%d" % (h, o), align_bytes=64)
+        def quantize(codes, scales, c0, width, grouped):
             nc.vector.quantize_mx(
-                out=q_code[(h, o)][:].bitcast(FP8X4),
-                scales=q_scale[(h, o)][:],
+                out=codes[:, c0 : c0 + width].bitcast(FP8X4),
+                scales=scales[:, c0 : c0 + width],
                 in_=grouped[:].rearrange("p w j -> p (w j)"),
             )
 
-        def one_pass(acc, h, r, a, o):
-            cols = slice(NMM * a, NMM * (a + 1))
+        for o in range(PASSES):
+            quantize(q_code[o], q_scale[o], 0, HALF, cast_q(o, 0, HALF, nc.scalar.copy, "g0%d" % o))
+
+        col = keep.tile([P, 2, PACK], F32, name="col", tag="raw01", align_bytes=64)
+        nc.scalar.copy(col[:, 0, :], ts_turned[:, :, LIVE])
+        nc.scalar.copy(col[:, 1, :], kb_turned[:, :, LIVE])
+
+        quantize(q_code[0], q_scale[0], HALF, HALF, cast_q(0, HALF, HALF, nc.scalar.copy, "g10"))
+        late = [cast_q(1, c0, NMM, nc.vector.tensor_copy, "late%d" % c0) for c0 in (HALF, HALF + NMM)]
+        quantize(q_code[1], q_scale[1], HALF, NMM, late[0])
+        quantize(q_code[1], q_scale[1], HALF + NMM, NMM, late[1])
+
+        def one_pass(acc, r, c0, a, o):
+            cols = slice(c0 + NMM * a, c0 + NMM * (a + 1))
             nc.tensor.matmul_mx(
-                out=acc[:, cols],
+                out=acc[:, NMM * a : NMM * (a + 1)],
                 lhsT=k_code[:, o, 2 * P * r : 2 * P * (r + 1)].bitcast(FP4X4),
-                lhsT_scale=k_scale[o][:, P * r : P * (r + 1)],
-                rhs=q_code[(h, o)][:, cols].bitcast(FP8X4),
-                rhs_scale=q_scale[(h, o)][:, cols],
+                lhsT_scale=k_scale[:, o, P * r : P * (r + 1)],
+                rhs=q_code[o][:, cols].bitcast(FP8X4),
+                rhs_scale=q_scale[o][:, cols],
                 start=(o == 0),
                 stop=(o == PASSES - 1),
             )
@@ -144,33 +158,31 @@ def tile_attend_plw_tskb_kernel(tc, qT, k_words, k_scales, ts, kb, offs, out_0, 
         y_rows = out_0.rearrange("(p r) q -> p r q", r=PACK)
         y_words = out_1[0].rearrange("p q u -> p (q u)").bitcast(I32)
 
-        for h in range(2):
-            for o in range(PASSES):
-                last = (h, o) == (1, PASSES - 1)
-                quantize_q(h, o, cast_q(h, o, nc.vector.tensor_copy if last else nc.scalar.copy))
-
-        for h in range(2):
-            cols = slice(HALF * h, HALF * (h + 1))
-            acc = [psum.tile([P, HALF], F32, name="acc%d%d" % (h, r), tag="bank%d" % (4 * h + r)) for r in range(PACK)]
-            y = keep.tile([P, PACK, HALF], F32, name="y%d" % h)
+        chunks = [(0, HALF, "raw10", "late384"), (HALF, NMM, "y1", "yg1"), (HALF + NMM, NMM, "y2", "yg2")]
+        for i, (c0, width, y_tag, g_tag) in enumerate(chunks):
+            acc = [
+                psum.tile([P, width], F32, name="acc%d%d" % (i, r), tag="bank%d" % (4 * (i % 2) + r))
+                for r in range(PACK)
+            ]
+            y = keep.tile([P, PACK, width], F32, name="y%d" % i, tag=y_tag, align_bytes=64)
             for r in range(PACK):
-                one_pass(acc[r], h, r, 0, 0)
+                one_pass(acc[r], r, c0, 0, 0)
             for r in range(PACK):
-                one_pass(acc[r], h, r, 0, 1)
-                one_pass(acc[r], h, r, 1, 0)
-                one_pass(acc[r], h, r, 1, 1)
-                nc.scalar.activation(y[:, r, :], acc[r][:], SIGMOID, bias=kb_col[:, r : r + 1], scale=ts_col[:, r : r + 1])
-            nc.sync.dma_start(y_rows[:, :, cols], y[:])
-            y_grouped = keep.tile([P, HALF, PACK], BF16, name="y_grouped%d" % h, align_bytes=64)
+                one_pass(acc[r], r, c0, 0, 1)
+                for a in range(1, width // NMM):
+                    one_pass(acc[r], r, c0, a, 0)
+                    one_pass(acc[r], r, c0, a, 1)
+                nc.scalar.activation(y[:, r, :], acc[r][:], SIGMOID, bias=col[:, 1, r : r + 1], scale=col[:, 0, r : r + 1])
+            nc.sync.dma_start(y_rows[:, :, c0 : c0 + width], y[:])
+            y_grouped = keep.tile([P, width, PACK], BF16, name="y_grouped%d" % i, tag=g_tag, align_bytes=64)
             interleave(nc.vector.tensor_copy, y_grouped[:], y[:])
-            nc.vector.quantize_mx(
-                out=y_code[:, cols].bitcast(FP8X4),
-                scales=y_scale[:, cols],
-                in_=y_grouped[:].rearrange("p w j -> p (w j)"),
-            )
-            nc.sync.dma_start(y_words[:, cols], y_code[:, cols].bitcast(I32))
+            quantize(y_code, y_scale, c0, width, y_grouped)
+            if i == 1:
+                nc.sync.dma_start(y_words[:, 0 : c0 + width], y_code[:, 0 : c0 + width].bitcast(I32))
+        nc.sync.dma_start(y_words[:, NQ - NMM : NQ], y_code[:, NQ - NMM : NQ].bitcast(I32))
         for quad in range(4):
-            nc.scalar.dma_start(
+            queue = nc.scalar if quad < 2 else nc.sync
+            queue.dma_start(
                 out_2[0, 4 * quad : 4 * quad + 4, :].bitcast(I32),
                 y_scale[32 * quad : 32 * quad + 4, :].bitcast(I32),
             )

@@ -40,7 +40,7 @@ def tile_attend_plw_tskb_kernel(tc, qT, k_words, k_scales, ts, kb, offs, out_0, 
         nc.sync.dma_start(offsets[:], offs)
 
         scale_pool = keep.tile([P, T], U8, name="scale_pool", align_bytes=64)
-        ts_pool = keep.tile([P, T + 1], F32, name="ts_pool")
+        ts_pool = keep.tile([P, T + 1], F32, name="ts_pool", tag="ts", align_bytes=64)
         kb_pool = keep.tile([P, T], F32, name="kb_pool")
         nc.sync.dma_start(
             scale_pool[SROW:P, :].bitcast(I32),
@@ -48,9 +48,6 @@ def tile_attend_plw_tskb_kernel(tc, qT, k_words, k_scales, ts, kb, offs, out_0, 
         )
         nc.sync.dma_start(ts_pool[LIVE:P, 0:T], ts[0:1, :])
         nc.sync.dma_start(kb_pool[LIVE:P, :], kb[0:1, :])
-
-        word_pool = keep.tile([P, T], I32, name="word_pool", align_bytes=64)
-        nc.sync.dma_start(word_pool[:], k_words[0].rearrange("p t b -> p (t b)").bitcast(I32))
 
         q_raw = {}
 
@@ -61,6 +58,8 @@ def tile_attend_plw_tskb_kernel(tc, qT, k_words, k_scales, ts, kb, offs, out_0, 
             q_raw[(h, o)] = raw
 
         load_q(0, 0)
+        word_pool = keep.tile([P, T], I32, name="word_pool", tag="words", align_bytes=64)
+        nc.sync.dma_start(word_pool[:], k_words[0].rearrange("p t b -> p (t b)").bitcast(I32))
         load_q(0, 1)
         load_q(1, 0)
 
@@ -102,19 +101,10 @@ def tile_attend_plw_tskb_kernel(tc, qT, k_words, k_scales, ts, kb, offs, out_0, 
             )
 
         load_q(1, 1)
-
         kb_turned = turned(kb_pool, "kb", "bank7")
 
-        word_picked = keep.tile([P, N], U32, name="word_picked", align_bytes=64)
-        nc.vector.tensor_copy(word_picked[:], word_pool[:].bitcast(U32).indirect(offsets[:]))
-        k_code = keep.tile([P, PASSES, 2 * N], U8, name="k_code", align_bytes=64)
-        nc.vector.tensor_copy(
-            k_code[:].bitcast(U16).rearrange("p o (r s) -> p o s r", r=PACK),
-            word_picked[:].bitcast(U16).rearrange("p (s r o) -> p o s r", r=PACK, o=PASSES),
-        )
-
-        q_code = [keep.tile([P, NQ], U32, name="q_code%d" % o, align_bytes=64) for o in range(PASSES)]
-        q_scale = [keep.tile([P, NQ], U8, name="q_scale%d" % o, align_bytes=64) for o in range(PASSES)]
+        q_code = {}
+        q_scale = {}
 
         def cast_q(o, c0, width, engine_copy, tag):
             h, first = divmod(c0, HALF)
@@ -126,29 +116,63 @@ def tile_attend_plw_tskb_kernel(tc, qT, k_words, k_scales, ts, kb, offs, out_0, 
             nc.vector.quantize_mx(
                 out=codes[:, c0 : c0 + width].bitcast(FP8X4),
                 scales=scales[:, c0 : c0 + width],
-                in_=grouped[:].rearrange("p w j -> p (w j)"),
+                in_=grouped.rearrange("p w j -> p (w j)"),
             )
 
+        def quantize_q(o, c0, width, grouped, tag):
+            codes = keep.tile([P, width], U32, name="q_code%d_%d" % (o, c0), tag=tag, align_bytes=64)
+            scales = keep.tile([P, width], U8, name="q_scale%d_%d" % (o, c0), align_bytes=64)
+            quantize(codes, scales, 0, width, grouped)
+            for a in range(width // NMM):
+                q_code[(o, c0 + NMM * a)] = codes[:, NMM * a : NMM * (a + 1)]
+                q_scale[(o, c0 + NMM * a)] = scales[:, NMM * a : NMM * (a + 1)]
+
+        g00 = cast_q(0, 0, HALF, nc.scalar.copy, "g00")
+        quantize_q(0, 0, NMM, g00[:, 0:NMM, :], "c00")
+
+        for w in range(2):
+            idle = psum.tile([P, N], F32, name="idle%d" % w, tag="bank%d" % (4 + w))
+            nc.tensor.matmul_mx(
+                out=idle[:],
+                lhsT=q_code[(0, 0)].bitcast(FP8X4),
+                lhsT_scale=q_scale[(0, 0)],
+                rhs=word_pool[:, 0 : N // 2].bitcast(U8).bitcast(FP4X4),
+                rhs_scale=scale_dealt[:],
+                start=True,
+                stop=True,
+            )
+
+        word_picked = keep.tile([P, N], U32, name="word_picked", align_bytes=64)
+        nc.vector.tensor_copy(word_picked[:], word_pool[:].bitcast(U32).indirect(offsets[:]))
+        quantize_q(0, NMM, NMM, g00[:, NMM:HALF, :], "words")
+        halves = word_picked[:].bitcast(U16).rearrange("p (s r o) -> p o s r", r=PACK, o=PASSES)
+        k_code = []
         for o in range(PASSES):
-            quantize(q_code[o], q_scale[o], 0, HALF, cast_q(o, 0, HALF, nc.scalar.copy, "g0%d" % o))
+            parted = keep.tile([P, 2 * N], U8, name="k_code%d" % o, align_bytes=64)
+            nc.vector.tensor_copy(parted[:].bitcast(U16).rearrange("p (r s) -> p s r", r=PACK), halves[:, o, :, :])
+            k_code.append(parted)
 
-        col = keep.tile([P, 2, PACK], F32, name="col", tag="raw01", align_bytes=64)
-        nc.scalar.copy(col[:, 0, :], ts_turned[:, :, LIVE])
-        nc.scalar.copy(col[:, 1, :], kb_turned[:, :, LIVE])
+        g01 = cast_q(1, 0, HALF, nc.scalar.copy, "g01")
+        quantize_q(1, 0, NMM, g01[:, 0:NMM, :], "c01")
+        quantize_q(1, NMM, NMM, g01[:, NMM:HALF, :], "c02")
 
-        quantize(q_code[0], q_scale[0], HALF, HALF, cast_q(0, HALF, HALF, nc.scalar.copy, "g10"))
+        ts_col = keep.tile([P, PACK], F32, name="ts_col", tag="raw00", align_bytes=64)
+        nc.scalar.copy(ts_col[:], ts_turned[:, :, LIVE])
+        kb_col = keep.tile([P, PACK], F32, name="kb_col", tag="raw01", align_bytes=64)
+        nc.scalar.copy(kb_col[:], kb_turned[:, :, LIVE])
+
+        quantize_q(0, HALF, HALF, cast_q(0, HALF, HALF, nc.scalar.copy, "g10")[:], "c10")
         late = [cast_q(1, c0, NMM, nc.vector.tensor_copy, "late%d" % c0) for c0 in (HALF, HALF + NMM)]
-        quantize(q_code[1], q_scale[1], HALF, NMM, late[0])
-        quantize(q_code[1], q_scale[1], HALF + NMM, NMM, late[1])
+        quantize_q(1, HALF, NMM, late[0][:], "c11")
+        quantize_q(1, HALF + NMM, NMM, late[1][:], "c12")
 
         def one_pass(acc, r, c0, a, o):
-            cols = slice(c0 + NMM * a, c0 + NMM * (a + 1))
             nc.tensor.matmul_mx(
-                out=acc[:, NMM * a : NMM * (a + 1)],
-                lhsT=k_code[:, o, 2 * P * r : 2 * P * (r + 1)].bitcast(FP4X4),
+                out=acc[:],
+                lhsT=k_code[o][:, 2 * P * r : 2 * P * (r + 1)].bitcast(FP4X4),
                 lhsT_scale=k_scale[:, o, P * r : P * (r + 1)],
-                rhs=q_code[o][:, cols].bitcast(FP8X4),
-                rhs_scale=q_scale[o][:, cols],
+                rhs=q_code[(o, c0 + NMM * a)].bitcast(FP8X4),
+                rhs_scale=q_scale[(o, c0 + NMM * a)],
                 start=(o == 0),
                 stop=(o == PASSES - 1),
             )
@@ -158,28 +182,43 @@ def tile_attend_plw_tskb_kernel(tc, qT, k_words, k_scales, ts, kb, offs, out_0, 
         y_rows = out_0.rearrange("(p r) q -> p r q", r=PACK)
         y_words = out_1[0].rearrange("p q u -> p (q u)").bitcast(I32)
 
-        chunks = [(0, HALF, "raw10", "late384"), (HALF, NMM, "y1", "yg1"), (HALF + NMM, NMM, "y2", "yg2")]
-        for i, (c0, width, y_tag, g_tag) in enumerate(chunks):
-            acc = [
-                psum.tile([P, width], F32, name="acc%d%d" % (i, r), tag="bank%d" % (4 * (i % 2) + r))
-                for r in range(PACK)
-            ]
-            y = keep.tile([P, PACK, width], F32, name="y%d" % i, tag=y_tag, align_bytes=64)
-            for r in range(PACK):
-                one_pass(acc[r], r, c0, 0, 0)
-            for r in range(PACK):
-                one_pass(acc[r], r, c0, 0, 1)
-                for a in range(1, width // NMM):
-                    one_pass(acc[r], r, c0, a, 0)
-                    one_pass(acc[r], r, c0, a, 1)
-                nc.scalar.activation(y[:, r, :], acc[r][:], SIGMOID, bias=col[:, 1, r : r + 1], scale=col[:, 0, r : r + 1])
-            nc.sync.dma_start(y_rows[:, :, c0 : c0 + width], y[:])
-            y_grouped = keep.tile([P, width, PACK], BF16, name="y_grouped%d" % i, tag=g_tag, align_bytes=64)
-            interleave(nc.vector.tensor_copy, y_grouped[:], y[:])
-            quantize(y_code, y_scale, c0, width, y_grouped)
-            if i == 1:
-                nc.sync.dma_start(y_words[:, 0 : c0 + width], y_code[:, 0 : c0 + width].bitcast(I32))
-        nc.sync.dma_start(y_words[:, NQ - NMM : NQ], y_code[:, NQ - NMM : NQ].bitcast(I32))
+        def round_y(y, first, width, engine_copy, name, tag):
+            grouped = keep.tile([P, width, PACK], BF16, name=name, tag=tag, align_bytes=64)
+            interleave(engine_copy, grouped[:], y[:, :, first : first + width])
+            return grouped
+
+        for h in range(2):
+            c0 = HALF * h
+            units = [(r, a) for r in range(PACK) for a in range(2)]
+            acc = {
+                (r, a): psum.tile([P, NMM], F32, name="acc%d%d%d" % (h, r, a), tag="bank%d" % (2 * r + a))
+                for r, a in units
+            }
+            y = keep.tile([P, PACK, HALF], F32, name="y%d" % h, tag="raw10" if h == 0 else "y1", align_bytes=64)
+            if h == 0:
+                for r, a in units:
+                    one_pass(acc[(r, a)], r, c0, a, 0)
+            for r, a in units:
+                if h == 1:
+                    one_pass(acc[(r, a)], r, c0, a, 0)
+                one_pass(acc[(r, a)], r, c0, a, 1)
+                nc.scalar.activation(
+                    y[:, r, NMM * a : NMM * (a + 1)],
+                    acc[(r, a)][:],
+                    SIGMOID,
+                    bias=kb_col[:, r : r + 1],
+                    scale=ts_col[:, r : r + 1],
+                )
+                if r % 2 == 1 and a == 1:
+                    nc.sync.dma_start(y_rows[:, r - 1 : r + 1, c0 : c0 + HALF], y[:, r - 1 : r + 1, :])
+            if h == 0:
+                quantize(y_code, y_scale, 0, HALF, round_y(y, 0, HALF, nc.vector.tensor_copy, "yg0", "late384")[:])
+            else:
+                first = round_y(y, 0, NMM, nc.vector.tensor_copy, "yg1", "yg1")
+                second = round_y(y, NMM, NMM, nc.scalar.copy, "yg2", "yg2")
+                quantize(y_code, y_scale, HALF, NMM, first[:])
+                quantize(y_code, y_scale, HALF + NMM, NMM, second[:])
+            nc.sync.dma_start(y_words[:, c0 : c0 + HALF], y_code[:, c0 : c0 + HALF].bitcast(I32))
         for quad in range(4):
             queue = nc.scalar if quad < 2 else nc.sync
             queue.dma_start(

@@ -24,6 +24,7 @@ HALF = NQ // 2
 NMM = 128
 LIVE = P - 1
 SROW = 96
+SHARE = 64
 
 
 def interleave(engine_copy, dst, src):
@@ -49,19 +50,13 @@ def tile_attend_plw_tskb_kernel(tc, qT, k_words, k_scales, ts, kb, offs, out_0, 
         nc.sync.dma_start(ts_pool[LIVE:P, 0:T], ts[0:1, :])
         nc.sync.dma_start(kb_pool[LIVE:P, :], kb[0:1, :])
 
-        q_raw = {}
-
-        def load_q(h, o):
-            raw = keep.tile([P, PACK, HALF], F32, name="q_raw%d%d" % (h, o), tag="raw%d%d" % (h, o), align_bytes=64)
-            rows = qT[0, 512 * o : 512 * (o + 1), HALF * h : HALF * (h + 1)]
-            nc.sync.dma_start(raw[:], rows.rearrange("(p j) w -> p j w", j=PACK))
-            q_raw[(h, o)] = raw
-
-        load_q(0, 0)
+        q_rows = qT[0].rearrange("(o p j) w -> o p j w", o=PASSES, j=PACK)
+        raw0 = keep.tile([P, PACK, NQ], F32, name="raw0", tag="raw0", align_bytes=64)
+        nc.sync.dma_start(raw0[:], q_rows[0])
         word_pool = keep.tile([P, T], I32, name="word_pool", tag="words", align_bytes=64)
         nc.sync.dma_start(word_pool[:], k_words[0].rearrange("p t b -> p (t b)").bitcast(I32))
-        load_q(0, 1)
-        load_q(1, 0)
+        raw1a = keep.tile([P, PACK, HALF], F32, name="raw1a", tag="raw1a", align_bytes=64)
+        nc.sync.dma_start(raw1a[:], q_rows[1][:, :, 0:HALF])
 
         k_scale = keep.tile([P, PASSES, N], U8, name="k_scale", align_bytes=64)
         nc.gpsimd.memset(scale_pool[0:SROW, :].bitcast(I32), 0)
@@ -76,7 +71,7 @@ def tile_attend_plw_tskb_kernel(tc, qT, k_words, k_scales, ts, kb, offs, out_0, 
         make_identity(nc, ident[:])
         nc.gpsimd.memset(k_scale[:].rearrange("p o n -> p (o n)").bitcast(I32), 0)
 
-        scale_picked = keep.tile([P, N], U8, name="scale_picked", tag="raw11", align_bytes=64)
+        scale_picked = keep.tile([P, N], U8, name="scale_picked", tag="raw1b", align_bytes=64)
         nc.vector.tensor_copy(scale_picked[:], scale_pool[:].indirect(offsets[:]))
 
         def turned(pool_tile, name, bank):
@@ -100,17 +95,17 @@ def tile_attend_plw_tskb_kernel(tc, qT, k_words, k_scales, ts, kb, offs, out_0, 
                 scale_dealt[SROW + 8 * quad : SROW + 8 * quad + 8, :].bitcast(I32),
             )
 
-        load_q(1, 1)
+        raw1b = keep.tile([P, PACK, HALF], F32, name="raw1b", tag="raw1b", align_bytes=64)
+        nc.sync.dma_start(raw1b[:], q_rows[1][:, :, HALF:NQ])
         kb_turned = turned(kb_pool, "kb", "bank7")
 
         q_code = {}
         q_scale = {}
 
-        def cast_q(o, c0, width, engine_copy, tag):
-            h, first = divmod(c0, HALF)
-            grouped = keep.tile([P, width, PACK], BF16, name="q_grouped%d_%d" % (o, c0), tag=tag, align_bytes=64)
-            interleave(engine_copy, grouped[:], q_raw[(h, o)][:, :, first : first + width])
-            return grouped
+        def rounded(src, engine_copy, name, tag):
+            grouped = keep.tile([P, src.shape[2], PACK], BF16, name=name, tag=tag, align_bytes=64)
+            interleave(engine_copy, grouped[:], src)
+            return grouped[:]
 
         def quantize(codes, scales, c0, width, grouped):
             nc.vector.quantize_mx(
@@ -127,24 +122,18 @@ def tile_attend_plw_tskb_kernel(tc, qT, k_words, k_scales, ts, kb, offs, out_0, 
                 q_code[(o, c0 + NMM * a)] = codes[:, NMM * a : NMM * (a + 1)]
                 q_scale[(o, c0 + NMM * a)] = scales[:, NMM * a : NMM * (a + 1)]
 
-        g00 = cast_q(0, 0, HALF, nc.scalar.copy, "g00")
-        quantize_q(0, 0, NMM, g00[:, 0:NMM, :], "c00")
-
-        for w in range(2):
-            idle = psum.tile([P, N], F32, name="idle%d" % w, tag="bank%d" % (4 + w))
-            nc.tensor.matmul_mx(
-                out=idle[:],
-                lhsT=q_code[(0, 0)].bitcast(FP8X4),
-                lhsT_scale=q_scale[(0, 0)],
-                rhs=word_pool[:, 0 : N // 2].bitcast(U8).bitcast(FP4X4),
-                rhs_scale=scale_dealt[:],
-                start=True,
-                stop=True,
-            )
+        g0a = rounded(raw0[:, :, 0:HALF], nc.scalar.copy, "g0a", "g0a")
+        quantize_q(0, 0, NMM, g0a[:, 0:NMM, :], "c0a")
+        g0b = rounded(raw0[:, :, HALF:NQ], nc.scalar.copy, "g0b", "g0b")
+        col = keep.tile([P, 2, PACK], F32, name="col", tag="raw0", align_bytes=64)
+        ts_col = col[:, 0, :]
+        kb_col = col[:, 1, :]
+        nc.scalar.copy(ts_col, ts_turned[:, :, LIVE])
+        nc.scalar.copy(kb_col, kb_turned[:, :, LIVE])
 
         word_picked = keep.tile([P, N], U32, name="word_picked", align_bytes=64)
         nc.vector.tensor_copy(word_picked[:], word_pool[:].bitcast(U32).indirect(offsets[:]))
-        quantize_q(0, NMM, NMM, g00[:, NMM:HALF, :], "words")
+        quantize_q(0, NMM, NMM, g0a[:, NMM:HALF, :], "words")
         halves = word_picked[:].bitcast(U16).rearrange("p (s r o) -> p o s r", r=PACK, o=PASSES)
         k_code = []
         for o in range(PASSES):
@@ -152,19 +141,16 @@ def tile_attend_plw_tskb_kernel(tc, qT, k_words, k_scales, ts, kb, offs, out_0, 
             nc.vector.tensor_copy(parted[:].bitcast(U16).rearrange("p (r s) -> p s r", r=PACK), halves[:, o, :, :])
             k_code.append(parted)
 
-        g01 = cast_q(1, 0, HALF, nc.scalar.copy, "g01")
-        quantize_q(1, 0, NMM, g01[:, 0:NMM, :], "c01")
-        quantize_q(1, NMM, NMM, g01[:, NMM:HALF, :], "c02")
-
-        ts_col = keep.tile([P, PACK], F32, name="ts_col", tag="raw00", align_bytes=64)
-        nc.scalar.copy(ts_col[:], ts_turned[:, :, LIVE])
-        kb_col = keep.tile([P, PACK], F32, name="kb_col", tag="raw01", align_bytes=64)
-        nc.scalar.copy(kb_col[:], kb_turned[:, :, LIVE])
-
-        quantize_q(0, HALF, HALF, cast_q(0, HALF, HALF, nc.scalar.copy, "g10")[:], "c10")
-        late = [cast_q(1, c0, NMM, nc.vector.tensor_copy, "late%d" % c0) for c0 in (HALF, HALF + NMM)]
-        quantize_q(1, HALF, NMM, late[0][:], "c11")
-        quantize_q(1, HALF + NMM, NMM, late[1][:], "c12")
+        for a in range(2):
+            name = "g1a%d" % a
+            quantize_q(1, NMM * a, NMM, rounded(raw1a[:, :, NMM * a : NMM * (a + 1)], nc.scalar.copy, name, name), "c" + name)
+        quantize_q(0, HALF, HALF, g0b, "g1a1")
+        late = [
+            rounded(raw1b[:, :, NMM * a : NMM * (a + 1)], nc.vector.tensor_copy, "late%d" % a, "late%d" % a)
+            for a in range(2)
+        ]
+        for a in range(2):
+            quantize_q(1, HALF + NMM * a, NMM, late[a], "clate%d" % a)
 
         def one_pass(acc, r, c0, a, o):
             nc.tensor.matmul_mx(
@@ -182,43 +168,49 @@ def tile_attend_plw_tskb_kernel(tc, qT, k_words, k_scales, ts, kb, offs, out_0, 
         y_rows = out_0.rearrange("(p r) q -> p r q", r=PACK)
         y_words = out_1[0].rearrange("p q u -> p (q u)").bitcast(I32)
 
-        def round_y(y, first, width, engine_copy, name, tag):
-            grouped = keep.tile([P, width, PACK], BF16, name=name, tag=tag, align_bytes=64)
-            interleave(engine_copy, grouped[:], y[:, :, first : first + width])
-            return grouped
+        def weigh(acc, y, r, a):
+            nc.scalar.activation(
+                y[:, r, NMM * a : NMM * (a + 1)],
+                acc[:],
+                SIGMOID,
+                bias=kb_col[:, r : r + 1],
+                scale=ts_col[:, r : r + 1],
+            )
 
-        for h in range(2):
-            c0 = HALF * h
-            units = [(r, a) for r in range(PACK) for a in range(2)]
-            acc = {
-                (r, a): psum.tile([P, NMM], F32, name="acc%d%d%d" % (h, r, a), tag="bank%d" % (2 * r + a))
-                for r, a in units
-            }
-            y = keep.tile([P, PACK, HALF], F32, name="y%d" % h, tag="raw10" if h == 0 else "y1", align_bytes=64)
-            if h == 0:
-                for r, a in units:
-                    one_pass(acc[(r, a)], r, c0, a, 0)
-            for r, a in units:
-                if h == 1:
-                    one_pass(acc[(r, a)], r, c0, a, 0)
-                one_pass(acc[(r, a)], r, c0, a, 1)
-                nc.scalar.activation(
-                    y[:, r, NMM * a : NMM * (a + 1)],
-                    acc[(r, a)][:],
-                    SIGMOID,
-                    bias=kb_col[:, r : r + 1],
-                    scale=ts_col[:, r : r + 1],
-                )
-                if r % 2 == 1 and a == 1:
-                    nc.sync.dma_start(y_rows[:, r - 1 : r + 1, c0 : c0 + HALF], y[:, r - 1 : r + 1, :])
-            if h == 0:
-                quantize(y_code, y_scale, 0, HALF, round_y(y, 0, HALF, nc.vector.tensor_copy, "yg0", "late384")[:])
+        def bank(name, index):
+            return psum.tile([P, NMM], F32, name=name, tag="bank%d" % index)
+
+        units = [(r, a) for r in range(PACK) for a in range(2)]
+        acc = [bank("acc0_%d" % i, i) for i in range(8)]
+        y = keep.tile([P, PACK, HALF], F32, name="y0", tag="raw1a", align_bytes=64)
+        for i, (r, a) in enumerate(units):
+            one_pass(acc[i], r, 0, a, 0)
+        for i, (r, a) in enumerate(units):
+            one_pass(acc[i], r, 0, a, 1)
+            weigh(acc[i], y, r, a)
+            if r % 2 == 1 and a == 1:
+                nc.sync.dma_start(y_rows[:, r - 1 : r + 1, 0:HALF], y[:, r - 1 : r + 1, :])
+        quantize(y_code, y_scale, 0, HALF, rounded(y[:], nc.vector.tensor_copy, "yg0", "late1"))
+        nc.sync.dma_start(y_words[:, 0:HALF], y_code[:, 0:HALF].bitcast(I32))
+
+        for a in range(2):
+            c0 = HALF + NMM * a
+            acc = [bank("acc1_%d%d" % (a, r), PACK * a + r) for r in range(PACK)]
+            y = keep.tile([P, PACK, NMM], F32, name="y1_%d" % a, align_bytes=64)
+            for r in range(PACK):
+                one_pass(acc[r], r, c0, 0, 0)
+            for r in range(PACK):
+                one_pass(acc[r], r, c0, 0, 1)
+                weigh(acc[r], y, r, 0)
+            nc.sync.dma_start(y_rows[:, :, c0 : c0 + NMM], y[:])
+            grouped = keep.tile([P, NMM, PACK], BF16, name="yg1_%d" % a, align_bytes=64)
+            if a == 0:
+                interleave(nc.vector.tensor_copy, grouped[:], y[:])
             else:
-                first = round_y(y, 0, NMM, nc.vector.tensor_copy, "yg1", "yg1")
-                second = round_y(y, NMM, NMM, nc.scalar.copy, "yg2", "yg2")
-                quantize(y_code, y_scale, HALF, NMM, first[:])
-                quantize(y_code, y_scale, HALF + NMM, NMM, second[:])
-            nc.sync.dma_start(y_words[:, c0 : c0 + HALF], y_code[:, c0 : c0 + HALF].bitcast(I32))
+                interleave(nc.vector.tensor_copy, grouped[:, 0:SHARE, :], y[:, :, 0:SHARE])
+                interleave(nc.scalar.copy, grouped[:, SHARE:NMM, :], y[:, :, SHARE:NMM])
+            quantize(y_code, y_scale, c0, NMM, grouped[:])
+        nc.sync.dma_start(y_words[:, HALF:NQ], y_code[:, HALF:NQ].bitcast(I32))
         for quad in range(4):
             queue = nc.scalar if quad < 2 else nc.sync
             queue.dma_start(

@@ -41,7 +41,7 @@ def tile_attend_plw_tskb_kernel(tc, qT, k_words, k_scales, ts, kb, offs, out_0, 
         nc.sync.dma_start(offsets[:], offs)
 
         scale_pool = keep.tile([P, T], U8, name="scale_pool", align_bytes=64)
-        ts_pool = keep.tile([P, T + 1], F32, name="ts_pool", tag="ts", align_bytes=64)
+        ts_pool = keep.tile([P, T + 1], F32, name="ts_pool", tag="raw1b", align_bytes=64)
         kb_pool = keep.tile([P, T], F32, name="kb_pool")
         nc.sync.dma_start(
             scale_pool[SROW:P, :].bitcast(I32),
@@ -55,8 +55,6 @@ def tile_attend_plw_tskb_kernel(tc, qT, k_words, k_scales, ts, kb, offs, out_0, 
         nc.sync.dma_start(raw0[:], q_rows[0])
         word_pool = keep.tile([P, T], I32, name="word_pool", tag="words", align_bytes=64)
         nc.sync.dma_start(word_pool[:], k_words[0].rearrange("p t b -> p (t b)").bitcast(I32))
-        raw1a = keep.tile([P, PACK, HALF], F32, name="raw1a", tag="raw1a", align_bytes=64)
-        nc.sync.dma_start(raw1a[:], q_rows[1][:, :, 0:HALF])
 
         k_scale = keep.tile([P, PASSES, N], U8, name="k_scale", align_bytes=64)
         nc.gpsimd.memset(scale_pool[0:SROW, :].bitcast(I32), 0)
@@ -71,18 +69,14 @@ def tile_attend_plw_tskb_kernel(tc, qT, k_words, k_scales, ts, kb, offs, out_0, 
         make_identity(nc, ident[:])
         nc.gpsimd.memset(k_scale[:].rearrange("p o n -> p (o n)").bitcast(I32), 0)
 
-        scale_picked = keep.tile([P, N], U8, name="scale_picked", tag="raw1b", align_bytes=64)
+        scale_picked = keep.tile([P, N], U8, name="scale_picked", tag="raw1a", align_bytes=64)
         nc.vector.tensor_copy(scale_picked[:], scale_pool[:].indirect(offsets[:]))
 
-        def turned(pool_tile, name, bank):
-            picked = keep.tile([P, N], F32, name=name + "_picked")
-            nc.vector.tensor_copy(picked[:], pool_tile[:, 0:T].indirect(offsets[:]))
-            out = psum.tile([P, PACK, P], F32, name=name + "_turned", tag=bank)
-            for r in range(PACK):
-                nc.tensor.transpose(out[:, r, :], picked[:, r:N:PACK], ident[:])
-            return out
-
-        ts_turned = turned(ts_pool, "ts", "bank6")
+        ts_picked = keep.tile([P, N], F32, name="ts_picked")
+        nc.vector.tensor_copy(ts_picked[:], ts_pool[:, 0:T].indirect(offsets[:]))
+        ts_turned = psum.tile([P, PACK, P], F32, name="ts_turned", tag="bank6")
+        for r in range(PACK):
+            nc.tensor.transpose(ts_turned[:, r, :], ts_picked[:, r:N:PACK], ident[:])
 
         scale_dealt = keep.tile([P, N], U8, name="scale_dealt", align_bytes=64)
         nc.vector.tensor_copy(
@@ -95,9 +89,12 @@ def tile_attend_plw_tskb_kernel(tc, qT, k_words, k_scales, ts, kb, offs, out_0, 
                 scale_dealt[SROW + 8 * quad : SROW + 8 * quad + 8, :].bitcast(I32),
             )
 
+        raw1a = keep.tile([P, PACK, HALF], F32, name="raw1a", tag="raw1a", align_bytes=64)
+        nc.sync.dma_start(raw1a[:], q_rows[1][:, :, 0:HALF])
         raw1b = keep.tile([P, PACK, HALF], F32, name="raw1b", tag="raw1b", align_bytes=64)
         nc.sync.dma_start(raw1b[:], q_rows[1][:, :, HALF:NQ])
-        kb_turned = turned(kb_pool, "kb", "bank7")
+        kb_picked = keep.tile([P, N], F32, name="kb_picked")
+        nc.vector.tensor_copy(kb_picked[:], kb_pool[:].indirect(offsets[:]))
 
         q_code = {}
         q_scale = {}
@@ -125,11 +122,14 @@ def tile_attend_plw_tskb_kernel(tc, qT, k_words, k_scales, ts, kb, offs, out_0, 
         g0a = rounded(raw0[:, :, 0:HALF], nc.scalar.copy, "g0a", "g0a")
         quantize_q(0, 0, NMM, g0a[:, 0:NMM, :], "c0a")
         g0b = rounded(raw0[:, :, HALF:NQ], nc.scalar.copy, "g0b", "g0b")
-        col = keep.tile([P, 2, PACK], F32, name="col", tag="raw0", align_bytes=64)
-        ts_col = col[:, 0, :]
-        kb_col = col[:, 1, :]
+        after_raw0 = keep.tile([P, N + PACK], F32, name="after_raw0", tag="raw0", align_bytes=64)
+        kb_dealt = after_raw0[:, 0:N]
+        ts_col = after_raw0[:, N : N + PACK]
+        nc.scalar.copy(kb_dealt.rearrange("p (r s) -> p s r", r=PACK), kb_picked[:].rearrange("p (s r) -> p s r", r=PACK))
+        kb_turned = psum.tile([P, PACK, P], F32, name="kb_turned", tag="bank7")
+        for r in range(PACK):
+            nc.tensor.transpose(kb_turned[:, r, :], kb_dealt[:, P * r : P * (r + 1)], ident[:])
         nc.scalar.copy(ts_col, ts_turned[:, :, LIVE])
-        nc.scalar.copy(kb_col, kb_turned[:, :, LIVE])
 
         word_picked = keep.tile([P, N], U32, name="word_picked", align_bytes=64)
         nc.vector.tensor_copy(word_picked[:], word_pool[:].bitcast(U32).indirect(offsets[:]))
@@ -144,6 +144,8 @@ def tile_attend_plw_tskb_kernel(tc, qT, k_words, k_scales, ts, kb, offs, out_0, 
         for a in range(2):
             name = "g1a%d" % a
             quantize_q(1, NMM * a, NMM, rounded(raw1a[:, :, NMM * a : NMM * (a + 1)], nc.scalar.copy, name, name), "c" + name)
+        kb_col = keep.tile([P, PACK], F32, name="kb_col", tag="raw1a", align_bytes=64)
+        nc.scalar.copy(kb_col[:], kb_turned[:, :, LIVE])
         quantize_q(0, HALF, HALF, g0b, "g1a1")
         late = [
             rounded(raw1b[:, :, NMM * a : NMM * (a + 1)], nc.vector.tensor_copy, "late%d" % a, "late%d" % a)
@@ -182,7 +184,7 @@ def tile_attend_plw_tskb_kernel(tc, qT, k_words, k_scales, ts, kb, offs, out_0, 
 
         units = [(r, a) for r in range(PACK) for a in range(2)]
         acc = [bank("acc0_%d" % i, i) for i in range(8)]
-        y = keep.tile([P, PACK, HALF], F32, name="y0", tag="raw1a", align_bytes=64)
+        y = keep.tile([P, PACK, HALF], F32, name="y0", align_bytes=64)
         for i, (r, a) in enumerate(units):
             one_pass(acc[i], r, 0, a, 0)
         for i, (r, a) in enumerate(units):

@@ -35,13 +35,14 @@ def tile_attend_plw_tskb_kernel(tc, qT, k_words, k_scales, ts, kb, offs, out_0, 
     nc = tc.nc
     with ExitStack() as ctx:
         keep = ctx.enter_context(tc.tile_pool(name="keep", bufs=1))
+        placed = ctx.enter_context(tc.tile_pool(name="placed", bufs=1))
         psum = ctx.enter_context(tc.psum_pool(name="psum", bufs=1))
 
         offsets = keep.tile([P, N // 16], U16, name="offsets")
         nc.sync.dma_start(offsets[:], offs)
 
         scale_pool = keep.tile([P, T], U8, name="scale_pool", align_bytes=64)
-        ts_pool = keep.tile([P, T + 1], F32, name="ts_pool", tag="raw1b", align_bytes=64)
+        ts_pool = keep.tile([P, T + 1], F32, name="ts_pool", align_bytes=64)
         kb_pool = keep.tile([P, T], F32, name="kb_pool")
         nc.sync.dma_start(
             scale_pool[SROW:P, :].bitcast(I32),
@@ -50,11 +51,11 @@ def tile_attend_plw_tskb_kernel(tc, qT, k_words, k_scales, ts, kb, offs, out_0, 
         nc.sync.dma_start(ts_pool[LIVE:P, 0:T], ts[0:1, :])
         nc.sync.dma_start(kb_pool[LIVE:P, :], kb[0:1, :])
 
-        q_rows = qT[0].rearrange("(o p j) w -> o p j w", o=PASSES, j=PACK)
-        raw0 = keep.tile([P, PACK, NQ], F32, name="raw0", tag="raw0", align_bytes=64)
-        nc.sync.dma_start(raw0[:], q_rows[0])
         word_pool = keep.tile([P, T], I32, name="word_pool", tag="words", align_bytes=64)
         nc.sync.dma_start(word_pool[:], k_words[0].rearrange("p t b -> p (t b)").bitcast(I32))
+        q_rows = qT[0].rearrange("(o p j) w -> o p j w", o=PASSES, j=PACK)
+        raw0 = keep.tile([P, PACK, NQ], F32, name="raw0", align_bytes=64)
+        nc.sync.dma_start(raw0[:], q_rows[0])
 
         k_scale = keep.tile([P, PASSES, N], U8, name="k_scale", align_bytes=64)
         nc.gpsimd.memset(scale_pool[0:SROW, :].bitcast(I32), 0)
@@ -69,7 +70,8 @@ def tile_attend_plw_tskb_kernel(tc, qT, k_words, k_scales, ts, kb, offs, out_0, 
         make_identity(nc, ident[:])
         nc.gpsimd.memset(k_scale[:].rearrange("p o n -> p (o n)").bitcast(I32), 0)
 
-        scale_picked = keep.tile([P, N], U8, name="scale_picked", tag="raw1a", align_bytes=64)
+        half_bytes = 4 * PACK * HALF
+        scale_picked = placed.tile([P, N], U8, name="scale_picked", offset=half_bytes - N // 2, align_bytes=64)
         nc.vector.tensor_copy(scale_picked[:], scale_pool[:].indirect(offsets[:]))
 
         ts_picked = keep.tile([P, N], F32, name="ts_picked")
@@ -89,18 +91,37 @@ def tile_attend_plw_tskb_kernel(tc, qT, k_words, k_scales, ts, kb, offs, out_0, 
                 scale_dealt[SROW + 8 * quad : SROW + 8 * quad + 8, :].bitcast(I32),
             )
 
-        raw1a = keep.tile([P, PACK, HALF], F32, name="raw1a", tag="raw1a", align_bytes=64)
+        raw1a = placed.tile([P, PACK, HALF], F32, name="raw1a", offset=0, align_bytes=64)
         nc.sync.dma_start(raw1a[:], q_rows[1][:, :, 0:HALF])
-        raw1b = keep.tile([P, PACK, HALF], F32, name="raw1b", tag="raw1b", align_bytes=64)
+        raw1b = placed.tile([P, PACK, HALF], F32, name="raw1b", offset=half_bytes, align_bytes=64)
         nc.sync.dma_start(raw1b[:], q_rows[1][:, :, HALF:NQ])
+
         kb_picked = keep.tile([P, N], F32, name="kb_picked")
         nc.vector.tensor_copy(kb_picked[:], kb_pool[:].indirect(offsets[:]))
+        ts_col = keep.tile([P, PACK], F32, name="ts_col")
+        nc.scalar.copy(ts_col[:], ts_turned[:, :, LIVE])
+        kb_dealt = keep.tile([P, N], F32, name="kb_dealt")
+        nc.scalar.copy(
+            kb_dealt[:].rearrange("p (r s) -> p s r", r=PACK), kb_picked[:].rearrange("p (s r) -> p s r", r=PACK)
+        )
+        kb_turned = psum.tile([P, PACK, P], F32, name="kb_turned", tag="bank7")
+        for r in range(PACK):
+            nc.tensor.transpose(kb_turned[:, r, :], kb_dealt[:, P * r : P * (r + 1)], ident[:])
+
+        word_picked = keep.tile([P, N], U32, name="word_picked", tag="picked", align_bytes=64)
+        nc.vector.tensor_copy(word_picked[:], word_pool[:].bitcast(U32).indirect(offsets[:]))
+        halves = word_picked[:].bitcast(U16).rearrange("p (s r o) -> p o s r", r=PACK, o=PASSES)
+        k_code = []
+        for o in range(PASSES):
+            parted = keep.tile([P, 2 * N], U8, name="k_code%d" % o, align_bytes=64)
+            nc.vector.tensor_copy(parted[:].bitcast(U16).rearrange("p (r s) -> p s r", r=PACK), halves[:, o, :, :])
+            k_code.append(parted)
 
         q_code = {}
         q_scale = {}
 
-        def rounded(src, engine_copy, name, tag):
-            grouped = keep.tile([P, src.shape[2], PACK], BF16, name=name, tag=tag, align_bytes=64)
+        def rounded(src, engine_copy, name, pool=keep, **place):
+            grouped = pool.tile([P, src.shape[2], PACK], BF16, name=name, align_bytes=64, **place)
             interleave(engine_copy, grouped[:], src)
             return grouped[:]
 
@@ -111,58 +132,44 @@ def tile_attend_plw_tskb_kernel(tc, qT, k_words, k_scales, ts, kb, offs, out_0, 
                 in_=grouped.rearrange("p w j -> p (w j)"),
             )
 
-        def quantize_q(o, c0, width, grouped, tag):
-            codes = keep.tile([P, width], U32, name="q_code%d_%d" % (o, c0), tag=tag, align_bytes=64)
-            scales = keep.tile([P, width], U8, name="q_scale%d_%d" % (o, c0), align_bytes=64)
-            quantize(codes, scales, 0, width, grouped)
-            for a in range(width // NMM):
-                q_code[(o, c0 + NMM * a)] = codes[:, NMM * a : NMM * (a + 1)]
-                q_scale[(o, c0 + NMM * a)] = scales[:, NMM * a : NMM * (a + 1)]
+        def quantize_q(o, chunk, grouped, **place):
+            codes = keep.tile([P, NMM], U32, name="q_code%d_%d" % (o, chunk), align_bytes=64, **place)
+            scales = keep.tile([P, NMM], U8, name="q_scale%d_%d" % (o, chunk), align_bytes=64)
+            quantize(codes, scales, 0, NMM, grouped)
+            q_code[(o, chunk)] = codes[:]
+            q_scale[(o, chunk)] = scales[:]
 
-        g0a = rounded(raw0[:, :, 0:HALF], nc.scalar.copy, "g0a", "g0a")
-        quantize_q(0, 0, NMM, g0a[:, 0:NMM, :], "c0a")
-        g0b = rounded(raw0[:, :, HALF:NQ], nc.scalar.copy, "g0b", "g0b")
-        after_raw0 = keep.tile([P, N + PACK], F32, name="after_raw0", tag="raw0", align_bytes=64)
-        kb_dealt = after_raw0[:, 0:N]
-        ts_col = after_raw0[:, N : N + PACK]
-        nc.scalar.copy(kb_dealt.rearrange("p (r s) -> p s r", r=PACK), kb_picked[:].rearrange("p (s r) -> p s r", r=PACK))
-        kb_turned = psum.tile([P, PACK, P], F32, name="kb_turned", tag="bank7")
-        for r in range(PACK):
-            nc.tensor.transpose(kb_turned[:, r, :], kb_dealt[:, P * r : P * (r + 1)], ident[:])
-        nc.scalar.copy(ts_col, ts_turned[:, :, LIVE])
+        def cols(raw, a):
+            return raw[:, :, NMM * a : NMM * (a + 1)]
 
-        word_picked = keep.tile([P, N], U32, name="word_picked", align_bytes=64)
-        nc.vector.tensor_copy(word_picked[:], word_pool[:].bitcast(U32).indirect(offsets[:]))
-        quantize_q(0, NMM, NMM, g0a[:, NMM:HALF, :], "words")
-        halves = word_picked[:].bitcast(U16).rearrange("p (s r o) -> p o s r", r=PACK, o=PASSES)
-        k_code = []
-        for o in range(PASSES):
-            parted = keep.tile([P, 2 * N], U8, name="k_code%d" % o, align_bytes=64)
-            nc.vector.tensor_copy(parted[:].bitcast(U16).rearrange("p (r s) -> p s r", r=PACK), halves[:, o, :, :])
-            k_code.append(parted)
-
-        for a in range(2):
-            name = "g1a%d" % a
-            quantize_q(1, NMM * a, NMM, rounded(raw1a[:, :, NMM * a : NMM * (a + 1)], nc.scalar.copy, name, name), "c" + name)
-        kb_col = keep.tile([P, PACK], F32, name="kb_col", tag="raw1a", align_bytes=64)
+        g00 = rounded(cols(raw0, 0), nc.scalar.copy, "g00")
+        g01 = rounded(cols(raw0, 1), nc.scalar.copy, "g01")
+        kb_col = keep.tile([P, PACK], F32, name="kb_col")
         nc.scalar.copy(kb_col[:], kb_turned[:, :, LIVE])
-        quantize_q(0, HALF, HALF, g0b, "g1a1")
-        late = [
-            rounded(raw1b[:, :, NMM * a : NMM * (a + 1)], nc.vector.tensor_copy, "late%d" % a, "late%d" % a)
-            for a in range(2)
-        ]
-        for a in range(2):
-            quantize_q(1, HALF + NMM * a, NMM, late[a], "clate%d" % a)
+        quantize_q(0, 0, g00, tag="words")
+        g03 = rounded(cols(raw0, 3), nc.vector.tensor_copy, "g03", tag="picked")
+        quantize_q(0, 1, g01)
+        g10 = rounded(cols(raw1a, 0), nc.scalar.copy, "g10")
+        g11 = rounded(cols(raw1a, 1), nc.vector.tensor_copy, "g11")
+        g02 = rounded(cols(raw0, 2), nc.scalar.copy, "g02", pool=placed, offset=0)
+        quantize_q(1, 1, g11)
+        quantize_q(1, 0, g10)
+        quantize_q(0, 3, g03)
+        quantize_q(0, 2, g02)
+        g12 = rounded(cols(raw1b, 0), nc.vector.tensor_copy, "g12")
+        g13 = rounded(cols(raw1b, 1), nc.vector.tensor_copy, "g13")
+        quantize_q(1, 2, g12)
+        quantize_q(1, 3, g13)
 
-        def one_pass(acc, r, c0, a, o):
+        def one_pass(acc, r, chunk, o, start, stop):
             nc.tensor.matmul_mx(
-                out=acc[:],
+                out=acc,
                 lhsT=k_code[o][:, 2 * P * r : 2 * P * (r + 1)].bitcast(FP4X4),
                 lhsT_scale=k_scale[:, o, P * r : P * (r + 1)],
-                rhs=q_code[(o, c0 + NMM * a)].bitcast(FP8X4),
-                rhs_scale=q_scale[(o, c0 + NMM * a)],
-                start=(o == 0),
-                stop=(o == PASSES - 1),
+                rhs=q_code[(o, chunk)].bitcast(FP8X4),
+                rhs_scale=q_scale[(o, chunk)],
+                start=start,
+                stop=stop,
             )
 
         y_code = keep.tile([P, NQ], U32, name="y_code", align_bytes=64)
@@ -170,43 +177,39 @@ def tile_attend_plw_tskb_kernel(tc, qT, k_words, k_scales, ts, kb, offs, out_0, 
         y_rows = out_0.rearrange("(p r) q -> p r q", r=PACK)
         y_words = out_1[0].rearrange("p q u -> p (q u)").bitcast(I32)
 
-        def weigh(acc, y, r, a):
-            nc.scalar.activation(
-                y[:, r, NMM * a : NMM * (a + 1)],
-                acc[:],
-                SIGMOID,
-                bias=kb_col[:, r : r + 1],
-                scale=ts_col[:, r : r + 1],
-            )
+        def weigh(acc, y, r):
+            nc.scalar.activation(y[:, r, :], acc, SIGMOID, bias=kb_col[:, r : r + 1], scale=ts_col[:, r : r + 1])
 
-        def bank(name, index):
-            return psum.tile([P, NMM], F32, name=name, tag="bank%d" % index)
-
-        units = [(r, a) for r in range(PACK) for a in range(2)]
-        acc = [bank("acc0_%d" % i, i) for i in range(8)]
+        acc = [psum.tile([P, HALF], F32, name="acc0_%d" % r, tag="bank%d" % r) for r in range(PACK)]
         y = keep.tile([P, PACK, HALF], F32, name="y0", align_bytes=64)
-        for i, (r, a) in enumerate(units):
-            one_pass(acc[i], r, 0, a, 0)
-        for i, (r, a) in enumerate(units):
-            one_pass(acc[i], r, 0, a, 1)
-            weigh(acc[i], y, r, a)
-            if r % 2 == 1 and a == 1:
+        for a in range(2):
+            for r in range(PACK):
+                one_pass(acc[r][:, NMM * a : NMM * (a + 1)], r, a, 0, a == 0, False)
+        for r in range(PACK):
+            for a in (1, 0):
+                one_pass(acc[r][:, NMM * a : NMM * (a + 1)], r, a, 1, False, a == 0)
+            weigh(acc[r][:], y, r)
+            if r % 2 == 1:
                 nc.sync.dma_start(y_rows[:, r - 1 : r + 1, 0:HALF], y[:, r - 1 : r + 1, :])
-        quantize(y_code, y_scale, 0, HALF, rounded(y[:], nc.vector.tensor_copy, "yg0", "late1"))
+        quantize(y_code, y_scale, 0, HALF, rounded(y[:], nc.vector.tensor_copy, "yg0"))
         nc.sync.dma_start(y_words[:, 0:HALF], y_code[:, 0:HALF].bitcast(I32))
 
-        for a in range(2):
-            c0 = HALF + NMM * a
-            acc = [bank("acc1_%d%d" % (a, r), PACK * a + r) for r in range(PACK)]
-            y = keep.tile([P, PACK, NMM], F32, name="y1_%d" % a, align_bytes=64)
+        for chunk in (2, 3):
+            c0 = NMM * chunk
+            first_bank = PACK * (3 - chunk)
+            acc = [
+                psum.tile([P, NMM], F32, name="acc%d_%d" % (chunk, r), tag="bank%d" % (first_bank + r))
+                for r in range(PACK)
+            ]
+            y = keep.tile([P, PACK, NMM], F32, name="y1_%d" % chunk, align_bytes=64)
             for r in range(PACK):
-                one_pass(acc[r], r, c0, 0, 0)
+                one_pass(acc[r][:], r, chunk, 0, True, False)
             for r in range(PACK):
-                one_pass(acc[r], r, c0, 0, 1)
-                weigh(acc[r], y, r, 0)
+                one_pass(acc[r][:], r, chunk, 1, False, True)
+                weigh(acc[r][:], y, r)
             nc.sync.dma_start(y_rows[:, :, c0 : c0 + NMM], y[:])
-            grouped = keep.tile([P, NMM, PACK], BF16, name="yg1_%d" % a, align_bytes=64)
-            if a == 0:
+            grouped = keep.tile([P, NMM, PACK], BF16, name="yg1_%d" % chunk, align_bytes=64)
+            if chunk == 2:
                 interleave(nc.vector.tensor_copy, grouped[:], y[:])
             else:
                 interleave(nc.vector.tensor_copy, grouped[:, 0:SHARE, :], y[:, :, 0:SHARE])

@@ -56,6 +56,8 @@ def tile_attend_plw_tskb_kernel(tc, qT, k_words, k_scales, ts, kb, offs, out_0, 
         q_rows = qT[0].rearrange("(o p j) w -> o p j w", o=PASSES, j=PACK)
         raw0 = keep.tile([P, PACK, NQ], F32, name="raw0", align_bytes=64)
         nc.sync.dma_start(raw0[:], q_rows[0])
+        raw1a = keep.tile([P, PACK, HALF], F32, name="raw1a", tag="raw1a", align_bytes=64)
+        nc.sync.dma_start(raw1a[:], q_rows[1][:, :, 0:HALF])
 
         k_scale = keep.tile([P, PASSES, N], U8, name="k_scale", align_bytes=64)
         nc.gpsimd.memset(scale_pool[0:SROW, :].bitcast(I32), 0)
@@ -65,20 +67,23 @@ def tile_attend_plw_tskb_kernel(tc, qT, k_words, k_scales, ts, kb, offs, out_0, 
         warm_out = keep.tile([P, 8], F32, name="warm_out")
         nc.gpsimd.memset(warm[:], 0.0)
         nc.scalar.activation(warm_out[:], warm[:], SIGMOID)
-        nc.gpsimd.memset(kb_pool[0:LIVE, :], 0.0)
         ident = keep.tile([P, P], F32, name="ident")
         make_identity(nc, ident[:])
+        nc.gpsimd.memset(kb_pool[0:LIVE, :], 0.0)
         nc.gpsimd.memset(k_scale[:].rearrange("p o n -> p (o n)").bitcast(I32), 0)
 
-        half_bytes = 4 * PACK * HALF
-        scale_picked = placed.tile([P, N], U8, name="scale_picked", offset=half_bytes - N // 2, align_bytes=64)
+        scale_picked = keep.tile([P, N], U8, name="scale_picked", tag="raw1b", align_bytes=64)
         nc.vector.tensor_copy(scale_picked[:], scale_pool[:].indirect(offsets[:]))
 
         ts_picked = keep.tile([P, N], F32, name="ts_picked")
         nc.vector.tensor_copy(ts_picked[:], ts_pool[:, 0:T].indirect(offsets[:]))
+        ts_dealt = keep.tile([P, N], F32, name="ts_dealt")
+        nc.scalar.copy(
+            ts_dealt[:].rearrange("p (r s) -> p s r", r=PACK), ts_picked[:].rearrange("p (s r) -> p s r", r=PACK)
+        )
         ts_turned = psum.tile([P, PACK, P], F32, name="ts_turned", tag="bank6")
         for r in range(PACK):
-            nc.tensor.transpose(ts_turned[:, r, :], ts_picked[:, r:N:PACK], ident[:])
+            nc.tensor.transpose(ts_turned[:, r, :], ts_dealt[:, P * r : P * (r + 1)], ident[:])
 
         scale_dealt = keep.tile([P, N], U8, name="scale_dealt", align_bytes=64)
         nc.vector.tensor_copy(
@@ -91,31 +96,22 @@ def tile_attend_plw_tskb_kernel(tc, qT, k_words, k_scales, ts, kb, offs, out_0, 
                 scale_dealt[SROW + 8 * quad : SROW + 8 * quad + 8, :].bitcast(I32),
             )
 
-        raw1a = placed.tile([P, PACK, HALF], F32, name="raw1a", offset=0, align_bytes=64)
-        nc.sync.dma_start(raw1a[:], q_rows[1][:, :, 0:HALF])
-        raw1b = placed.tile([P, PACK, HALF], F32, name="raw1b", offset=half_bytes, align_bytes=64)
+        raw1b = keep.tile([P, PACK, HALF], F32, name="raw1b", tag="raw1b", align_bytes=64)
         nc.sync.dma_start(raw1b[:], q_rows[1][:, :, HALF:NQ])
 
         kb_picked = keep.tile([P, N], F32, name="kb_picked")
         nc.vector.tensor_copy(kb_picked[:], kb_pool[:].indirect(offsets[:]))
-        ts_col = keep.tile([P, PACK], F32, name="ts_col")
-        nc.scalar.copy(ts_col[:], ts_turned[:, :, LIVE])
-        kb_dealt = keep.tile([P, N], F32, name="kb_dealt")
-        nc.scalar.copy(
-            kb_dealt[:].rearrange("p (r s) -> p s r", r=PACK), kb_picked[:].rearrange("p (s r) -> p s r", r=PACK)
-        )
         kb_turned = psum.tile([P, PACK, P], F32, name="kb_turned", tag="bank7")
         for r in range(PACK):
-            nc.tensor.transpose(kb_turned[:, r, :], kb_dealt[:, P * r : P * (r + 1)], ident[:])
+            nc.tensor.transpose(kb_turned[:, r, :], kb_picked[:, r:N:PACK], ident[:])
 
         word_picked = keep.tile([P, N], U32, name="word_picked", tag="picked", align_bytes=64)
         nc.vector.tensor_copy(word_picked[:], word_pool[:].bitcast(U32).indirect(offsets[:]))
         halves = word_picked[:].bitcast(U16).rearrange("p (s r o) -> p o s r", r=PACK, o=PASSES)
-        k_code = []
-        for o in range(PASSES):
-            parted = keep.tile([P, 2 * N], U8, name="k_code%d" % o, align_bytes=64)
-            nc.vector.tensor_copy(parted[:].bitcast(U16).rearrange("p (r s) -> p s r", r=PACK), halves[:, o, :, :])
-            k_code.append(parted)
+        k_code = [keep.tile([P, 2 * N], U8, name="k_code%d" % o, align_bytes=64) for o in range(PASSES)]
+
+        def part(o):
+            nc.vector.tensor_copy(k_code[o][:].bitcast(U16).rearrange("p (r s) -> p s r", r=PACK), halves[:, o, :, :])
 
         q_code = {}
         q_scale = {}
@@ -133,33 +129,37 @@ def tile_attend_plw_tskb_kernel(tc, qT, k_words, k_scales, ts, kb, offs, out_0, 
             )
 
         def quantize_q(o, chunk, grouped, **place):
-            codes = keep.tile([P, NMM], U32, name="q_code%d_%d" % (o, chunk), align_bytes=64, **place)
-            scales = keep.tile([P, NMM], U8, name="q_scale%d_%d" % (o, chunk), align_bytes=64)
-            quantize(codes, scales, 0, NMM, grouped)
-            q_code[(o, chunk)] = codes[:]
-            q_scale[(o, chunk)] = scales[:]
+            width = grouped.shape[1]
+            codes = keep.tile([P, width], U32, name="q_code%d_%d" % (o, chunk), align_bytes=64, **place)
+            scales = keep.tile([P, width], U8, name="q_scale%d_%d" % (o, chunk), align_bytes=64)
+            quantize(codes, scales, 0, width, grouped)
+            for a in range(width // NMM):
+                q_code[(o, chunk + a)] = codes[:, NMM * a : NMM * (a + 1)]
+                q_scale[(o, chunk + a)] = scales[:, NMM * a : NMM * (a + 1)]
 
         def cols(raw, a):
             return raw[:, :, NMM * a : NMM * (a + 1)]
 
-        g00 = rounded(cols(raw0, 0), nc.scalar.copy, "g00")
-        g01 = rounded(cols(raw0, 1), nc.scalar.copy, "g01")
-        kb_col = keep.tile([P, PACK], F32, name="kb_col")
-        nc.scalar.copy(kb_col[:], kb_turned[:, :, LIVE])
+        g00 = rounded(cols(raw0, 0), nc.scalar.copy, "g00", pool=placed, offset=0)
+        g01 = rounded(cols(raw0, 1), nc.scalar.copy, "g01", tag="g01")
+        part(0)
         quantize_q(0, 0, g00, tag="words")
-        g03 = rounded(cols(raw0, 3), nc.vector.tensor_copy, "g03", tag="picked")
+        part(1)
+        columns = placed.tile([P, 2, PACK], F32, name="columns", offset=0, align_bytes=64)
+        ts_col = columns[:, 0, :]
+        kb_col = columns[:, 1, :]
+        nc.scalar.copy(ts_col, ts_turned[:, :, LIVE])
+        nc.scalar.copy(kb_col, kb_turned[:, :, LIVE])
+        g1a = placed.tile([P, HALF, PACK], BF16, name="g1a", offset=960, align_bytes=64)
+        interleave(nc.scalar.copy, g1a[:, 0:NMM, :], cols(raw1a, 0))
+        interleave(nc.vector.tensor_copy, g1a[:, NMM:HALF, :], cols(raw1a, 1))
         quantize_q(0, 1, g01)
-        g10 = rounded(cols(raw1a, 0), nc.scalar.copy, "g10")
-        g11 = rounded(cols(raw1a, 1), nc.vector.tensor_copy, "g11")
-        g02 = rounded(cols(raw0, 2), nc.scalar.copy, "g02", pool=placed, offset=0)
-        quantize_q(1, 1, g11)
-        quantize_q(1, 0, g10)
-        quantize_q(0, 3, g03)
-        quantize_q(0, 2, g02)
-        g12 = rounded(cols(raw1b, 0), nc.vector.tensor_copy, "g12")
-        g13 = rounded(cols(raw1b, 1), nc.vector.tensor_copy, "g13")
-        quantize_q(1, 2, g12)
-        quantize_q(1, 3, g13)
+        quantize_q(1, 1, g1a[:, NMM:HALF, :])
+        quantize_q(1, 0, g1a[:, 0:NMM, :])
+        g0b = rounded(raw0[:, :, HALF:NQ], nc.scalar.copy, "g0b", tag="raw1a")
+        g1b = rounded(raw1b[:], nc.vector.tensor_copy, "g1b", tag="g01")
+        quantize_q(0, 2, g0b, tag="raw1b")
+        quantize_q(1, 2, g1b)
 
         def one_pass(acc, r, chunk, o, start, stop):
             nc.tensor.matmul_mx(
@@ -178,43 +178,44 @@ def tile_attend_plw_tskb_kernel(tc, qT, k_words, k_scales, ts, kb, offs, out_0, 
         y_words = out_1[0].rearrange("p q u -> p (q u)").bitcast(I32)
 
         def weigh(acc, y, r):
-            nc.scalar.activation(y[:, r, :], acc, SIGMOID, bias=kb_col[:, r : r + 1], scale=ts_col[:, r : r + 1])
+            nc.scalar.activation(y, acc, SIGMOID, bias=kb_col[:, r : r + 1], scale=ts_col[:, r : r + 1])
 
         acc = [psum.tile([P, HALF], F32, name="acc0_%d" % r, tag="bank%d" % r) for r in range(PACK)]
-        y = keep.tile([P, PACK, HALF], F32, name="y0", align_bytes=64)
+        ya = keep.tile([P, PACK, HALF], F32, name="ya", align_bytes=64)
         for a in range(2):
             for r in range(PACK):
                 one_pass(acc[r][:, NMM * a : NMM * (a + 1)], r, a, 0, a == 0, False)
         for r in range(PACK):
             for a in (1, 0):
                 one_pass(acc[r][:, NMM * a : NMM * (a + 1)], r, a, 1, False, a == 0)
-            weigh(acc[r][:], y, r)
+            weigh(acc[r][:], ya[:, r, :], r)
             if r % 2 == 1:
-                nc.sync.dma_start(y_rows[:, r - 1 : r + 1, 0:HALF], y[:, r - 1 : r + 1, :])
-        quantize(y_code, y_scale, 0, HALF, rounded(y[:], nc.vector.tensor_copy, "yg0"))
-        nc.sync.dma_start(y_words[:, 0:HALF], y_code[:, 0:HALF].bitcast(I32))
+                nc.sync.dma_start(y_rows[:, r - 1 : r + 1, 0:HALF], ya[:, r - 1 : r + 1, :])
 
-        for chunk in (2, 3):
-            c0 = NMM * chunk
-            first_bank = PACK * (3 - chunk)
+        yb = keep.tile([P, PACK, HALF], F32, name="yb", align_bytes=64)
+        for a in range(2):
+            first_bank = PACK * (1 - a)
             acc = [
-                psum.tile([P, NMM], F32, name="acc%d_%d" % (chunk, r), tag="bank%d" % (first_bank + r))
+                psum.tile([P, NMM], F32, name="acc1_%d%d" % (a, r), tag="bank%d" % (first_bank + r))
                 for r in range(PACK)
             ]
-            y = keep.tile([P, PACK, NMM], F32, name="y1_%d" % chunk, align_bytes=64)
             for r in range(PACK):
-                one_pass(acc[r][:], r, chunk, 0, True, False)
+                one_pass(acc[r][:], r, 2 + a, 0, True, False)
             for r in range(PACK):
-                one_pass(acc[r][:], r, chunk, 1, False, True)
-                weigh(acc[r][:], y, r)
-            nc.sync.dma_start(y_rows[:, :, c0 : c0 + NMM], y[:])
-            grouped = keep.tile([P, NMM, PACK], BF16, name="yg1_%d" % chunk, align_bytes=64)
-            if chunk == 2:
-                interleave(nc.vector.tensor_copy, grouped[:], y[:])
-            else:
-                interleave(nc.vector.tensor_copy, grouped[:, 0:SHARE, :], y[:, :, 0:SHARE])
-                interleave(nc.scalar.copy, grouped[:, SHARE:NMM, :], y[:, :, SHARE:NMM])
-            quantize(y_code, y_scale, c0, NMM, grouped[:])
+                one_pass(acc[r][:], r, 2 + a, 1, False, True)
+                weigh(acc[r][:], yb[:, r, NMM * a : NMM * (a + 1)], r)
+                if a == 1 and r % 2 == 1:
+                    nc.sync.dma_start(y_rows[:, r - 1 : r + 1, HALF:NQ], yb[:, r - 1 : r + 1, :])
+
+        yga = rounded(ya[:], nc.vector.tensor_copy, "yga")
+        ygb = keep.tile([P, HALF, PACK], BF16, name="ygb", align_bytes=64)
+        interleave(nc.vector.tensor_copy, ygb[:, 0:NMM, :], cols(yb, 0))
+        quantize(y_code, y_scale, 0, HALF, yga)
+        nc.sync.dma_start(y_words[:, 0:HALF], y_code[:, 0:HALF].bitcast(I32))
+        cut = NMM + SHARE
+        interleave(nc.vector.tensor_copy, ygb[:, NMM:cut, :], yb[:, :, NMM:cut])
+        interleave(nc.scalar.copy, ygb[:, cut:HALF, :], yb[:, :, cut:HALF])
+        quantize(y_code, y_scale, HALF, HALF, ygb[:])
         nc.sync.dma_start(y_words[:, HALF:NQ], y_code[:, HALF:NQ].bitcast(I32))
         for quad in range(4):
             queue = nc.scalar if quad < 2 else nc.sync

@@ -24,7 +24,9 @@ HALF = NQ // 2
 NMM = 128
 LIVE = P - 1
 SROW = 96
-SHARE = 64
+SHARE = 160
+RAW1_AT = 0
+HALF_BYTES = 4 * PACK * HALF
 
 
 def interleave(engine_copy, dst, src):
@@ -51,13 +53,11 @@ def tile_attend_plw_tskb_kernel(tc, qT, k_words, k_scales, ts, kb, offs, out_0, 
         nc.sync.dma_start(ts_pool[LIVE:P, 0:T], ts[0:1, :])
         nc.sync.dma_start(kb_pool[LIVE:P, :], kb[0:1, :])
 
-        word_pool = keep.tile([P, T], I32, name="word_pool", tag="words", align_bytes=64)
-        nc.sync.dma_start(word_pool[:], k_words[0].rearrange("p t b -> p (t b)").bitcast(I32))
         q_rows = qT[0].rearrange("(o p j) w -> o p j w", o=PASSES, j=PACK)
         raw0 = keep.tile([P, PACK, NQ], F32, name="raw0", align_bytes=64)
         nc.sync.dma_start(raw0[:], q_rows[0])
-        raw1a = keep.tile([P, PACK, HALF], F32, name="raw1a", tag="raw1a", align_bytes=64)
-        nc.sync.dma_start(raw1a[:], q_rows[1][:, :, 0:HALF])
+        word_pool = keep.tile([P, T], I32, name="word_pool", align_bytes=64)
+        nc.sync.dma_start(word_pool[:], k_words[0].rearrange("p t b -> p (t b)").bitcast(I32))
 
         k_scale = keep.tile([P, PASSES, N], U8, name="k_scale", align_bytes=64)
         nc.gpsimd.memset(scale_pool[0:SROW, :].bitcast(I32), 0)
@@ -72,18 +72,14 @@ def tile_attend_plw_tskb_kernel(tc, qT, k_words, k_scales, ts, kb, offs, out_0, 
         nc.gpsimd.memset(kb_pool[0:LIVE, :], 0.0)
         nc.gpsimd.memset(k_scale[:].rearrange("p o n -> p (o n)").bitcast(I32), 0)
 
-        scale_picked = keep.tile([P, N], U8, name="scale_picked", tag="raw1b", align_bytes=64)
+        scale_picked = placed.tile([P, N], U8, name="scale_picked", offset=RAW1_AT + HALF_BYTES - N // 2, align_bytes=64)
         nc.vector.tensor_copy(scale_picked[:], scale_pool[:].indirect(offsets[:]))
 
         ts_picked = keep.tile([P, N], F32, name="ts_picked")
         nc.vector.tensor_copy(ts_picked[:], ts_pool[:, 0:T].indirect(offsets[:]))
-        ts_dealt = keep.tile([P, N], F32, name="ts_dealt")
-        nc.scalar.copy(
-            ts_dealt[:].rearrange("p (r s) -> p s r", r=PACK), ts_picked[:].rearrange("p (s r) -> p s r", r=PACK)
-        )
         ts_turned = psum.tile([P, PACK, P], F32, name="ts_turned", tag="bank6")
         for r in range(PACK):
-            nc.tensor.transpose(ts_turned[:, r, :], ts_dealt[:, P * r : P * (r + 1)], ident[:])
+            nc.tensor.transpose(ts_turned[:, r, :], ts_picked[:, r:N:PACK], ident[:])
 
         scale_dealt = keep.tile([P, N], U8, name="scale_dealt", align_bytes=64)
         nc.vector.tensor_copy(
@@ -96,7 +92,9 @@ def tile_attend_plw_tskb_kernel(tc, qT, k_words, k_scales, ts, kb, offs, out_0, 
                 scale_dealt[SROW + 8 * quad : SROW + 8 * quad + 8, :].bitcast(I32),
             )
 
-        raw1b = keep.tile([P, PACK, HALF], F32, name="raw1b", tag="raw1b", align_bytes=64)
+        raw1a = placed.tile([P, PACK, HALF], F32, name="raw1a", offset=RAW1_AT, align_bytes=64)
+        nc.sync.dma_start(raw1a[:], q_rows[1][:, :, 0:HALF])
+        raw1b = placed.tile([P, PACK, HALF], F32, name="raw1b", offset=RAW1_AT + HALF_BYTES, align_bytes=64)
         nc.sync.dma_start(raw1b[:], q_rows[1][:, :, HALF:NQ])
 
         kb_picked = keep.tile([P, N], F32, name="kb_picked")
@@ -104,14 +102,6 @@ def tile_attend_plw_tskb_kernel(tc, qT, k_words, k_scales, ts, kb, offs, out_0, 
         kb_turned = psum.tile([P, PACK, P], F32, name="kb_turned", tag="bank7")
         for r in range(PACK):
             nc.tensor.transpose(kb_turned[:, r, :], kb_picked[:, r:N:PACK], ident[:])
-
-        word_picked = keep.tile([P, N], U32, name="word_picked", tag="picked", align_bytes=64)
-        nc.vector.tensor_copy(word_picked[:], word_pool[:].bitcast(U32).indirect(offsets[:]))
-        halves = word_picked[:].bitcast(U16).rearrange("p (s r o) -> p o s r", r=PACK, o=PASSES)
-        k_code = [keep.tile([P, 2 * N], U8, name="k_code%d" % o, align_bytes=64) for o in range(PASSES)]
-
-        def part(o):
-            nc.vector.tensor_copy(k_code[o][:].bitcast(U16).rearrange("p (r s) -> p s r", r=PACK), halves[:, o, :, :])
 
         q_code = {}
         q_scale = {}
@@ -128,9 +118,9 @@ def tile_attend_plw_tskb_kernel(tc, qT, k_words, k_scales, ts, kb, offs, out_0, 
                 in_=grouped.rearrange("p w j -> p (w j)"),
             )
 
-        def quantize_q(o, chunk, grouped, **place):
+        def quantize_q(o, chunk, grouped, pool=keep, **place):
             width = grouped.shape[1]
-            codes = keep.tile([P, width], U32, name="q_code%d_%d" % (o, chunk), align_bytes=64, **place)
+            codes = pool.tile([P, width], U32, name="q_code%d_%d" % (o, chunk), align_bytes=64, **place)
             scales = keep.tile([P, width], U8, name="q_scale%d_%d" % (o, chunk), align_bytes=64)
             quantize(codes, scales, 0, width, grouped)
             for a in range(width // NMM):
@@ -140,25 +130,43 @@ def tile_attend_plw_tskb_kernel(tc, qT, k_words, k_scales, ts, kb, offs, out_0, 
         def cols(raw, a):
             return raw[:, :, NMM * a : NMM * (a + 1)]
 
-        g00 = rounded(cols(raw0, 0), nc.scalar.copy, "g00", pool=placed, offset=0)
-        g01 = rounded(cols(raw0, 1), nc.scalar.copy, "g01", tag="g01")
-        part(0)
-        quantize_q(0, 0, g00, tag="words")
-        part(1)
-        columns = placed.tile([P, 2, PACK], F32, name="columns", offset=0, align_bytes=64)
+        g0a = rounded(raw0[:, :, 0:HALF], nc.scalar.copy, "g0a")
+        quantize_q(0, 0, g0a)
+        g0b = rounded(raw0[:, :, HALF:NQ], nc.scalar.copy, "g0b")
+
+        for i in range(2):
+            unread = psum.tile([P, N], F32, name="unread%d" % i, tag="bank%d" % (4 + i))
+            nc.tensor.matmul_mx(
+                out=unread[:],
+                lhsT=q_code[(0, i)].bitcast(FP8X4),
+                lhsT_scale=q_scale[(0, i)],
+                rhs=word_pool[:, 0 : N // 2].bitcast(U8).bitcast(FP4X4),
+                rhs_scale=scale_pool[:, 0:N],
+                start=True,
+                stop=True,
+            )
+
+        word_picked = keep.tile([P, N], U32, name="word_picked", tag="picked", align_bytes=64)
+        nc.vector.tensor_copy(word_picked[:], word_pool[:].bitcast(U32).indirect(offsets[:]))
+        halves = word_picked[:].bitcast(U16).rearrange("p (s r o) -> p o s r", r=PACK, o=PASSES)
+        k_code = []
+        for o in range(PASSES):
+            parted = keep.tile([P, 2 * N], U8, name="k_code%d" % o, align_bytes=64)
+            nc.vector.tensor_copy(parted[:].bitcast(U16).rearrange("p (r s) -> p s r", r=PACK), halves[:, o, :, :])
+            k_code.append(parted)
+        quantize_q(0, 2, g0b, tag="picked")
+
+        g1a = keep.tile([P, HALF, PACK], BF16, name="g1a", align_bytes=64)
+        interleave(nc.scalar.copy, g1a[:, 0:NMM, :], cols(raw1a, 0))
+        interleave(nc.vector.tensor_copy, g1a[:, NMM:HALF, :], cols(raw1a, 1))
+        columns = placed.tile([P, 2, PACK], F32, name="columns", offset=RAW1_AT + HALF_BYTES // 2, align_bytes=64)
         ts_col = columns[:, 0, :]
         kb_col = columns[:, 1, :]
         nc.scalar.copy(ts_col, ts_turned[:, :, LIVE])
         nc.scalar.copy(kb_col, kb_turned[:, :, LIVE])
-        g1a = placed.tile([P, HALF, PACK], BF16, name="g1a", offset=960, align_bytes=64)
-        interleave(nc.scalar.copy, g1a[:, 0:NMM, :], cols(raw1a, 0))
-        interleave(nc.vector.tensor_copy, g1a[:, NMM:HALF, :], cols(raw1a, 1))
-        quantize_q(0, 1, g01)
         quantize_q(1, 1, g1a[:, NMM:HALF, :])
         quantize_q(1, 0, g1a[:, 0:NMM, :])
-        g0b = rounded(raw0[:, :, HALF:NQ], nc.scalar.copy, "g0b", tag="raw1a")
-        g1b = rounded(raw1b[:], nc.vector.tensor_copy, "g1b", tag="g01")
-        quantize_q(0, 2, g0b, tag="raw1b")
+        g1b = rounded(raw1b[:], nc.vector.tensor_copy, "g1b", pool=placed, offset=RAW1_AT)
         quantize_q(1, 2, g1b)
 
         def one_pass(acc, r, chunk, o, start, stop):
@@ -180,43 +188,33 @@ def tile_attend_plw_tskb_kernel(tc, qT, k_words, k_scales, ts, kb, offs, out_0, 
         def weigh(acc, y, r):
             nc.scalar.activation(y, acc, SIGMOID, bias=kb_col[:, r : r + 1], scale=ts_col[:, r : r + 1])
 
-        acc = [psum.tile([P, HALF], F32, name="acc0_%d" % r, tag="bank%d" % r) for r in range(PACK)]
-        ya = keep.tile([P, PACK, HALF], F32, name="ya", align_bytes=64)
-        for a in range(2):
-            for r in range(PACK):
-                one_pass(acc[r][:, NMM * a : NMM * (a + 1)], r, a, 0, a == 0, False)
-        for r in range(PACK):
-            for a in (1, 0):
-                one_pass(acc[r][:, NMM * a : NMM * (a + 1)], r, a, 1, False, a == 0)
-            weigh(acc[r][:], ya[:, r, :], r)
-            if r % 2 == 1:
-                nc.sync.dma_start(y_rows[:, r - 1 : r + 1, 0:HALF], ya[:, r - 1 : r + 1, :])
+        acc = [psum.tile([P, HALF], F32, name="acc%d" % i, tag="bank%d" % i) for i in range(2 * PACK)]
 
-        yb = keep.tile([P, PACK, HALF], F32, name="yb", align_bytes=64)
-        for a in range(2):
-            first_bank = PACK * (1 - a)
-            acc = [
-                psum.tile([P, NMM], F32, name="acc1_%d%d" % (a, r), tag="bank%d" % (first_bank + r))
-                for r in range(PACK)
-            ]
-            for r in range(PACK):
-                one_pass(acc[r][:], r, 2 + a, 0, True, False)
-            for r in range(PACK):
-                one_pass(acc[r][:], r, 2 + a, 1, False, True)
-                weigh(acc[r][:], yb[:, r, NMM * a : NMM * (a + 1)], r)
-                if a == 1 and r % 2 == 1:
-                    nc.sync.dma_start(y_rows[:, r - 1 : r + 1, HALF:NQ], yb[:, r - 1 : r + 1, :])
+        def out_cols(chunk, r):
+            return acc[PACK * (chunk // 2) + r][:, NMM * (chunk % 2) : NMM * (chunk % 2 + 1)]
 
-        yga = rounded(ya[:], nc.vector.tensor_copy, "yga")
-        ygb = keep.tile([P, HALF, PACK], BF16, name="ygb", align_bytes=64)
-        interleave(nc.vector.tensor_copy, ygb[:, 0:NMM, :], cols(yb, 0))
-        quantize(y_code, y_scale, 0, HALF, yga)
-        nc.sync.dma_start(y_words[:, 0:HALF], y_code[:, 0:HALF].bitcast(I32))
-        cut = NMM + SHARE
-        interleave(nc.vector.tensor_copy, ygb[:, NMM:cut, :], yb[:, :, NMM:cut])
-        interleave(nc.scalar.copy, ygb[:, cut:HALF, :], yb[:, :, cut:HALF])
-        quantize(y_code, y_scale, HALF, HALF, ygb[:])
-        nc.sync.dma_start(y_words[:, HALF:NQ], y_code[:, HALF:NQ].bitcast(I32))
+        for chunk in range(2):
+            for r in range(PACK):
+                one_pass(out_cols(chunk, r), r, chunk, 0, chunk == 0, False)
+        for h in range(2):
+            y = keep.tile([P, PACK, HALF], F32, name="y%d" % h, align_bytes=64)
+            span = slice(HALF * h, HALF * (h + 1))
+            for r in range(PACK):
+                for chunk in range(2, 2 + 2 * h):
+                    one_pass(out_cols(chunk, r), r, chunk, 0, chunk == 2, False)
+                for chunk in (2 * h + 1, 2 * h):
+                    one_pass(out_cols(chunk, r), r, chunk, 1, False, chunk % 2 == 0)
+                weigh(acc[PACK * h + r][:], y[:, r, :], r)
+                if r % 2 == 1:
+                    nc.sync.dma_start(y_rows[:, r - 1 : r + 1, span], y[:, r - 1 : r + 1, :])
+            grouped = keep.tile([P, HALF, PACK], BF16, name="yg%d" % h, align_bytes=64)
+            if h == 0:
+                interleave(nc.vector.tensor_copy, grouped[:], y[:])
+            else:
+                interleave(nc.vector.tensor_copy, grouped[:, 0:SHARE, :], y[:, :, 0:SHARE])
+                interleave(nc.scalar.copy, grouped[:, SHARE:HALF, :], y[:, :, SHARE:HALF])
+            quantize(y_code, y_scale, HALF * h, HALF, grouped[:])
+            nc.sync.dma_start(y_words[:, span], y_code[:, span].bitcast(I32))
         for quad in range(4):
             queue = nc.scalar if quad < 2 else nc.sync
             queue.dma_start(

@@ -25,8 +25,7 @@ NMM = 128
 LIVE = P - 1
 SROW = 96
 SHARE = 160
-RAW1_AT = 0
-HALF_BYTES = 4 * PACK * HALF
+AHEAD = 2
 
 
 def interleave(engine_copy, dst, src):
@@ -37,7 +36,6 @@ def tile_attend_plw_tskb_kernel(tc, qT, k_words, k_scales, ts, kb, offs, out_0, 
     nc = tc.nc
     with ExitStack() as ctx:
         keep = ctx.enter_context(tc.tile_pool(name="keep", bufs=1))
-        placed = ctx.enter_context(tc.tile_pool(name="placed", bufs=1))
         psum = ctx.enter_context(tc.psum_pool(name="psum", bufs=1))
 
         offsets = keep.tile([P, N // 16], U16, name="offsets")
@@ -54,10 +52,12 @@ def tile_attend_plw_tskb_kernel(tc, qT, k_words, k_scales, ts, kb, offs, out_0, 
         nc.sync.dma_start(kb_pool[LIVE:P, :], kb[0:1, :])
 
         q_rows = qT[0].rearrange("(o p j) w -> o p j w", o=PASSES, j=PACK)
-        raw0 = keep.tile([P, PACK, NQ], F32, name="raw0", align_bytes=64)
+        raw0 = keep.tile([P, PACK, NQ], F32, name="raw0", tag="raw0", align_bytes=64)
         nc.sync.dma_start(raw0[:], q_rows[0])
-        word_pool = keep.tile([P, T], I32, name="word_pool", align_bytes=64)
+        word_pool = keep.tile([P, T], I32, name="word_pool", tag="words", align_bytes=64)
         nc.sync.dma_start(word_pool[:], k_words[0].rearrange("p t b -> p (t b)").bitcast(I32))
+        raw1a = keep.tile([P, PACK, HALF], F32, name="raw1a", tag="raw1a", align_bytes=64)
+        nc.sync.dma_start(raw1a[:], q_rows[1][:, :, 0:HALF])
 
         k_scale = keep.tile([P, PASSES, N], U8, name="k_scale", align_bytes=64)
         nc.gpsimd.memset(scale_pool[0:SROW, :].bitcast(I32), 0)
@@ -72,7 +72,7 @@ def tile_attend_plw_tskb_kernel(tc, qT, k_words, k_scales, ts, kb, offs, out_0, 
         nc.gpsimd.memset(kb_pool[0:LIVE, :], 0.0)
         nc.gpsimd.memset(k_scale[:].rearrange("p o n -> p (o n)").bitcast(I32), 0)
 
-        scale_picked = placed.tile([P, N], U8, name="scale_picked", offset=RAW1_AT + HALF_BYTES - N // 2, align_bytes=64)
+        scale_picked = keep.tile([P, N], U8, name="scale_picked", tag="raw1b", align_bytes=64)
         nc.vector.tensor_copy(scale_picked[:], scale_pool[:].indirect(offsets[:]))
 
         ts_picked = keep.tile([P, N], F32, name="ts_picked")
@@ -92,9 +92,7 @@ def tile_attend_plw_tskb_kernel(tc, qT, k_words, k_scales, ts, kb, offs, out_0, 
                 scale_dealt[SROW + 8 * quad : SROW + 8 * quad + 8, :].bitcast(I32),
             )
 
-        raw1a = placed.tile([P, PACK, HALF], F32, name="raw1a", offset=RAW1_AT, align_bytes=64)
-        nc.sync.dma_start(raw1a[:], q_rows[1][:, :, 0:HALF])
-        raw1b = placed.tile([P, PACK, HALF], F32, name="raw1b", offset=RAW1_AT + HALF_BYTES, align_bytes=64)
+        raw1b = keep.tile([P, PACK, HALF], F32, name="raw1b", tag="raw1b", align_bytes=64)
         nc.sync.dma_start(raw1b[:], q_rows[1][:, :, HALF:NQ])
 
         kb_picked = keep.tile([P, N], F32, name="kb_picked")
@@ -106,8 +104,8 @@ def tile_attend_plw_tskb_kernel(tc, qT, k_words, k_scales, ts, kb, offs, out_0, 
         q_code = {}
         q_scale = {}
 
-        def rounded(src, engine_copy, name, pool=keep, **place):
-            grouped = pool.tile([P, src.shape[2], PACK], BF16, name=name, align_bytes=64, **place)
+        def rounded(src, engine_copy, name, **place):
+            grouped = keep.tile([P, src.shape[2], PACK], BF16, name=name, align_bytes=64, **place)
             interleave(engine_copy, grouped[:], src)
             return grouped[:]
 
@@ -118,9 +116,9 @@ def tile_attend_plw_tskb_kernel(tc, qT, k_words, k_scales, ts, kb, offs, out_0, 
                 in_=grouped.rearrange("p w j -> p (w j)"),
             )
 
-        def quantize_q(o, chunk, grouped, pool=keep, **place):
+        def quantize_q(o, chunk, grouped, **place):
             width = grouped.shape[1]
-            codes = pool.tile([P, width], U32, name="q_code%d_%d" % (o, chunk), align_bytes=64, **place)
+            codes = keep.tile([P, width], U32, name="q_code%d_%d" % (o, chunk), align_bytes=64, **place)
             scales = keep.tile([P, width], U8, name="q_scale%d_%d" % (o, chunk), align_bytes=64)
             quantize(codes, scales, 0, width, grouped)
             for a in range(width // NMM):
@@ -154,19 +152,18 @@ def tile_attend_plw_tskb_kernel(tc, qT, k_words, k_scales, ts, kb, offs, out_0, 
             parted = keep.tile([P, 2 * N], U8, name="k_code%d" % o, align_bytes=64)
             nc.vector.tensor_copy(parted[:].bitcast(U16).rearrange("p (r s) -> p s r", r=PACK), halves[:, o, :, :])
             k_code.append(parted)
-        quantize_q(0, 2, g0b, tag="picked")
 
-        g1a = keep.tile([P, HALF, PACK], BF16, name="g1a", align_bytes=64)
-        interleave(nc.scalar.copy, g1a[:, 0:NMM, :], cols(raw1a, 0))
-        interleave(nc.vector.tensor_copy, g1a[:, NMM:HALF, :], cols(raw1a, 1))
-        columns = placed.tile([P, 2, PACK], F32, name="columns", offset=RAW1_AT + HALF_BYTES // 2, align_bytes=64)
+        columns = keep.tile([P, 2, PACK], F32, name="columns", tag="raw0", align_bytes=64)
         ts_col = columns[:, 0, :]
         kb_col = columns[:, 1, :]
         nc.scalar.copy(ts_col, ts_turned[:, :, LIVE])
         nc.scalar.copy(kb_col, kb_turned[:, :, LIVE])
-        quantize_q(1, 1, g1a[:, NMM:HALF, :])
-        quantize_q(1, 0, g1a[:, 0:NMM, :])
-        g1b = rounded(raw1b[:], nc.vector.tensor_copy, "g1b", pool=placed, offset=RAW1_AT)
+        g10 = rounded(cols(raw1a, 0), nc.scalar.copy, "g10")
+        g11 = rounded(cols(raw1a, 1), nc.vector.tensor_copy, "g11", tag="words")
+        quantize_q(0, 2, g0b, tag="picked")
+        quantize_q(1, 1, g11)
+        quantize_q(1, 0, g10)
+        g1b = rounded(raw1b[:], nc.vector.tensor_copy, "g1b", tag="raw1a")
         quantize_q(1, 2, g1b)
 
         def one_pass(acc, r, chunk, o, start, stop):
@@ -196,12 +193,16 @@ def tile_attend_plw_tskb_kernel(tc, qT, k_words, k_scales, ts, kb, offs, out_0, 
         for chunk in range(2):
             for r in range(PACK):
                 one_pass(out_cols(chunk, r), r, chunk, 0, chunk == 0, False)
+        for r in range(AHEAD):
+            for chunk in (2, 3):
+                one_pass(out_cols(chunk, r), r, chunk, 0, chunk == 2, False)
         for h in range(2):
             y = keep.tile([P, PACK, HALF], F32, name="y%d" % h, align_bytes=64)
             span = slice(HALF * h, HALF * (h + 1))
             for r in range(PACK):
-                for chunk in range(2, 2 + 2 * h):
-                    one_pass(out_cols(chunk, r), r, chunk, 0, chunk == 2, False)
+                if h == 1 and r >= AHEAD:
+                    for chunk in (2, 3):
+                        one_pass(out_cols(chunk, r), r, chunk, 0, chunk == 2, False)
                 for chunk in (2 * h + 1, 2 * h):
                     one_pass(out_cols(chunk, r), r, chunk, 1, False, chunk % 2 == 0)
                 weigh(acc[PACK * h + r][:], y[:, r, :], r)

@@ -16,16 +16,18 @@ U8 = mybir.dt.uint8
 FP8X4 = mybir.dt.float8_e4m3fn_x4
 FP4X4 = mybir.dt.float4_e2m1fn_x4
 SIGMOID = mybir.ActivationFunctionType.Sigmoid
+COPY = mybir.ActivationFunctionType.Copy
 
 P = 128
 PACK = 4
 PASSES = D // (P * PACK)
 HALF = NQ // 2
-NMM = 128
+CHUNK = 128
 LIVE = P - 1
-SROW = 96
+SROWS = 32
 SHARE = 160
 AHEAD = 2
+SHARE_Q = 160
 
 
 def interleave(engine_copy, dst, src):
@@ -36,115 +38,69 @@ def tile_attend_plw_tskb_kernel(tc, qT, k_words, k_scales, ts, kb, offs, out_0, 
     nc = tc.nc
     with ExitStack() as ctx:
         keep = ctx.enter_context(tc.tile_pool(name="keep", bufs=1))
+        relay = ctx.enter_context(tc.tile_pool(name="relay", bufs=1))
         psum = ctx.enter_context(tc.psum_pool(name="psum", bufs=1))
 
         offsets = keep.tile([P, N // 16], U16, name="offsets")
         nc.sync.dma_start(offsets[:], offs)
 
-        scale_pool = keep.tile([P, T], U8, name="scale_pool", align_bytes=64)
-        ts_pool = keep.tile([P, T + 1], F32, name="ts_pool", align_bytes=64)
-        kb_pool = keep.tile([P, T], F32, name="kb_pool")
+        half_bytes = 4 * PACK * HALF
+        scale_pool = relay.tile([P, T], U8, name="scale_pool", align_bytes=64, offset=half_bytes - T // 2)
+        ts_pool = keep.tile([P, T], F32, name="ts_pool", align_bytes=64)
+        kb_pool = keep.tile([P, T], F32, name="kb_pool", align_bytes=64)
         nc.sync.dma_start(
-            scale_pool[SROW:P, :].bitcast(I32),
+            scale_pool[0:SROWS, :].bitcast(I32),
             k_scales.rearrange("o f t -> f o t").bitcast(I32),
         )
-        nc.sync.dma_start(ts_pool[LIVE:P, 0:T], ts[0:1, :])
+        nc.sync.dma_start(ts_pool[LIVE:P, :], ts[0:1, :])
         nc.sync.dma_start(kb_pool[LIVE:P, :], kb[0:1, :])
-
+        word_pool = keep.tile([P, T], I32, name="word_pool", align_bytes=64)
+        nc.sync.dma_start(word_pool[:], k_words[0].rearrange("p t b -> p (t b)").bitcast(I32))
         q_rows = qT[0].rearrange("(o p j) w -> o p j w", o=PASSES, j=PACK)
         raw0 = keep.tile([P, PACK, NQ], F32, name="raw0", tag="raw0", align_bytes=64)
         nc.sync.dma_start(raw0[:], q_rows[0])
-        word_pool = keep.tile([P, T], I32, name="word_pool", tag="words", align_bytes=64)
-        nc.sync.dma_start(word_pool[:], k_words[0].rearrange("p t b -> p (t b)").bitcast(I32))
-        raw1a = keep.tile([P, PACK, HALF], F32, name="raw1a", tag="raw1a", align_bytes=64)
-        nc.sync.dma_start(raw1a[:], q_rows[1][:, :, 0:HALF])
-
-        k_scale = keep.tile([P, PASSES, N], U8, name="k_scale", align_bytes=64)
-        nc.gpsimd.memset(scale_pool[0:SROW, :].bitcast(I32), 0)
-        nc.vector.memset(ts_pool[0:LIVE, :], 0.0)
 
         warm = keep.tile([P, 8], F32, name="warm")
         warm_out = keep.tile([P, 8], F32, name="warm_out")
         nc.gpsimd.memset(warm[:], 0.0)
         nc.scalar.activation(warm_out[:], warm[:], SIGMOID)
+
+        nc.gpsimd.memset(scale_pool[SROWS : 2 * SROWS, :].bitcast(I32), 0)
+        nc.gpsimd.memset(scale_pool[2 * SROWS : P, :].bitcast(I32), 0)
+        nc.vector.memset(ts_pool[0:LIVE, 0 : T - 1], 0.0)
+        nc.vector.memset(ts_pool[0:LIVE, T - 1 : T], 0.0)
+        k_scale = keep.tile([P, PASSES, N], U8, name="k_scale", align_bytes=64)
+        nc.gpsimd.memset(k_scale[:].rearrange("p o n -> p (o n)").bitcast(I32), 0)
         ident = keep.tile([P, P], F32, name="ident")
         make_identity(nc, ident[:])
         nc.gpsimd.memset(kb_pool[0:LIVE, :], 0.0)
-        nc.gpsimd.memset(k_scale[:].rearrange("p o n -> p (o n)").bitcast(I32), 0)
-
-        scale_picked = keep.tile([P, N], U8, name="scale_picked", tag="raw1b", align_bytes=64)
-        nc.vector.tensor_copy(scale_picked[:], scale_pool[:].indirect(offsets[:]))
-
-        ts_picked = keep.tile([P, N], F32, name="ts_picked")
-        nc.vector.tensor_copy(ts_picked[:], ts_pool[:, 0:T].indirect(offsets[:]))
-        ts_turned = psum.tile([P, PACK, P], F32, name="ts_turned", tag="bank6")
-        for r in range(PACK):
-            nc.tensor.transpose(ts_turned[:, r, :], ts_picked[:, r:N:PACK], ident[:])
 
         scale_dealt = keep.tile([P, N], U8, name="scale_dealt", align_bytes=64)
         nc.vector.tensor_copy(
-            scale_dealt[:].rearrange("p (r s) -> p r s", r=PACK),
-            scale_picked[:].rearrange("p (s r) -> p r s", r=PACK),
+            scale_dealt[:].rearrange("p (r s) -> p s r", r=PACK),
+            scale_pool[:].indirect(offsets[:]),
         )
         for quad in range(4):
             nc.sync.dma_start(
                 k_scale[32 * quad : 32 * quad + 4, :, :].bitcast(I32),
-                scale_dealt[SROW + 8 * quad : SROW + 8 * quad + 8, :].bitcast(I32),
+                scale_dealt[8 * quad : 8 * quad + 8, :].bitcast(I32),
             )
+        raw1 = []
+        for h in range(2):
+            half = relay.tile([P, PACK, HALF], F32, name="raw1_%d" % h, align_bytes=64, offset=half_bytes * h)
+            nc.sync.dma_start(half[:], q_rows[1][:, :, HALF * h : HALF * (h + 1)])
+            raw1.append(half)
 
-        raw1b = keep.tile([P, PACK, HALF], F32, name="raw1b", tag="raw1b", align_bytes=64)
-        nc.sync.dma_start(raw1b[:], q_rows[1][:, :, HALF:NQ])
+        turned = []
+        for i, pool in enumerate((ts_pool, kb_pool)):
+            picked = keep.tile([P, N], F32, name="picked%d" % i)
+            nc.scalar.activation(picked[:], pool[:].indirect(offsets[:]), COPY)
+            bank = psum.tile([P, PACK, P], F32, name="turned%d" % i, tag="bank%d" % (6 + i))
+            for r in range(PACK):
+                nc.tensor.transpose(bank[:, r, :], picked[:, r:N:PACK], ident[:])
+            turned.append(bank)
 
-        kb_picked = keep.tile([P, N], F32, name="kb_picked")
-        nc.vector.tensor_copy(kb_picked[:], kb_pool[:].indirect(offsets[:]))
-        kb_turned = psum.tile([P, PACK, P], F32, name="kb_turned", tag="bank7")
-        for r in range(PACK):
-            nc.tensor.transpose(kb_turned[:, r, :], kb_picked[:, r:N:PACK], ident[:])
-
-        q_code = {}
-        q_scale = {}
-
-        def rounded(src, engine_copy, name, **place):
-            grouped = keep.tile([P, src.shape[2], PACK], BF16, name=name, align_bytes=64, **place)
-            interleave(engine_copy, grouped[:], src)
-            return grouped[:]
-
-        def quantize(codes, scales, c0, width, grouped):
-            nc.vector.quantize_mx(
-                out=codes[:, c0 : c0 + width].bitcast(FP8X4),
-                scales=scales[:, c0 : c0 + width],
-                in_=grouped.rearrange("p w j -> p (w j)"),
-            )
-
-        def quantize_q(o, chunk, grouped, **place):
-            width = grouped.shape[1]
-            codes = keep.tile([P, width], U32, name="q_code%d_%d" % (o, chunk), align_bytes=64, **place)
-            scales = keep.tile([P, width], U8, name="q_scale%d_%d" % (o, chunk), align_bytes=64)
-            quantize(codes, scales, 0, width, grouped)
-            for a in range(width // NMM):
-                q_code[(o, chunk + a)] = codes[:, NMM * a : NMM * (a + 1)]
-                q_scale[(o, chunk + a)] = scales[:, NMM * a : NMM * (a + 1)]
-
-        def cols(raw, a):
-            return raw[:, :, NMM * a : NMM * (a + 1)]
-
-        g0a = rounded(raw0[:, :, 0:HALF], nc.scalar.copy, "g0a")
-        quantize_q(0, 0, g0a)
-        g0b = rounded(raw0[:, :, HALF:NQ], nc.scalar.copy, "g0b")
-
-        for i in range(2):
-            unread = psum.tile([P, N], F32, name="unread%d" % i, tag="bank%d" % (4 + i))
-            nc.tensor.matmul_mx(
-                out=unread[:],
-                lhsT=q_code[(0, i)].bitcast(FP8X4),
-                lhsT_scale=q_scale[(0, i)],
-                rhs=word_pool[:, 0 : N // 2].bitcast(U8).bitcast(FP4X4),
-                rhs_scale=scale_pool[:, 0:N],
-                start=True,
-                stop=True,
-            )
-
-        word_picked = keep.tile([P, N], U32, name="word_picked", tag="picked", align_bytes=64)
+        word_picked = keep.tile([P, N], U32, name="word_picked", align_bytes=64)
         nc.vector.tensor_copy(word_picked[:], word_pool[:].bitcast(U32).indirect(offsets[:]))
         halves = word_picked[:].bitcast(U16).rearrange("p (s r o) -> p o s r", r=PACK, o=PASSES)
         k_code = []
@@ -153,26 +109,51 @@ def tile_attend_plw_tskb_kernel(tc, qT, k_words, k_scales, ts, kb, offs, out_0, 
             nc.vector.tensor_copy(parted[:].bitcast(U16).rearrange("p (r s) -> p s r", r=PACK), halves[:, o, :, :])
             k_code.append(parted)
 
-        columns = keep.tile([P, 2, PACK], F32, name="columns", tag="raw0", align_bytes=64)
-        ts_col = columns[:, 0, :]
-        kb_col = columns[:, 1, :]
-        nc.scalar.copy(ts_col, ts_turned[:, :, LIVE])
-        nc.scalar.copy(kb_col, kb_turned[:, :, LIVE])
-        g10 = rounded(cols(raw1a, 0), nc.scalar.copy, "g10")
-        g11 = rounded(cols(raw1a, 1), nc.vector.tensor_copy, "g11", tag="words")
-        quantize_q(0, 2, g0b, tag="picked")
-        quantize_q(1, 1, g11)
-        quantize_q(1, 0, g10)
-        g1b = rounded(raw1b[:], nc.vector.tensor_copy, "g1b", tag="raw1a")
-        quantize_q(1, 2, g1b)
+        ts_col = keep.tile([P, PACK], F32, name="ts_col")
+        nc.scalar.copy(ts_col[:], turned[0][:, :, LIVE])
 
-        def one_pass(acc, r, chunk, o, start, stop):
+        def rounded(src, engine_copy, name, **place):
+            grouped = keep.tile([P, src.shape[2], PACK], BF16, name=name, align_bytes=64, **place)
+            interleave(engine_copy, grouped[:], src)
+            return grouped[:]
+
+        def quantize(codes, scales, grouped):
+            nc.vector.quantize_mx(out=codes.bitcast(FP8X4), scales=scales, in_=grouped.rearrange("p w j -> p (w j)"))
+
+        def quantize_q(name, grouped, **place):
+            width = grouped.shape[1]
+            codes = keep.tile([P, width], U32, name=name + "_code", align_bytes=64, **place)
+            scales = keep.tile([P, width], U8, name=name + "_scale", align_bytes=64)
+            quantize(codes[:], scales[:], grouped)
+            return codes[:], scales[:]
+
+        def cols(raw, a):
+            return raw[:, :, CHUNK * a : CHUNK * (a + 1)]
+
+        g00 = rounded(cols(raw0, 0), nc.vector.tensor_copy, "g00")
+        g01 = rounded(cols(raw0, 1), nc.vector.tensor_copy, "g01")
+        g0b = rounded(raw0[:, :, HALF:NQ], nc.scalar.copy, "g0b")
+        q00 = quantize_q("q00", g00)
+        q01 = quantize_q("q01", g01)
+        kb_col = keep.tile([P, PACK], F32, name="kb_col", tag="raw0", align_bytes=64)
+        nc.scalar.copy(kb_col[:], turned[1][:, :, LIVE])
+        q0b = quantize_q("q0b", g0b)
+        g1a = keep.tile([P, HALF, PACK], BF16, name="g1a", align_bytes=64)
+        interleave(nc.vector.tensor_copy, g1a[:, 0:SHARE_Q, :], raw1[0][:, :, 0:SHARE_Q])
+        interleave(nc.scalar.copy, g1a[:, SHARE_Q:HALF, :], raw1[0][:, :, SHARE_Q:HALF])
+        q1a = quantize_q("q1a", g1a[:])
+        g12 = rounded(cols(raw1[1], 0), nc.vector.tensor_copy, "g12")
+        g13 = rounded(cols(raw1[1], 1), nc.vector.tensor_copy, "g13")
+        q12 = quantize_q("q12", g12)
+        q13 = quantize_q("q13", g13)
+
+        def one_pass(acc, r, o, q, start, stop):
             nc.tensor.matmul_mx(
                 out=acc,
                 lhsT=k_code[o][:, 2 * P * r : 2 * P * (r + 1)].bitcast(FP4X4),
                 lhsT_scale=k_scale[:, o, P * r : P * (r + 1)],
-                rhs=q_code[(o, chunk)].bitcast(FP8X4),
-                rhs_scale=q_scale[(o, chunk)],
+                rhs=q[0].bitcast(FP8X4),
+                rhs_scale=q[1],
                 start=start,
                 stop=stop,
             )
@@ -182,39 +163,42 @@ def tile_attend_plw_tskb_kernel(tc, qT, k_words, k_scales, ts, kb, offs, out_0, 
         y_rows = out_0.rearrange("(p r) q -> p r q", r=PACK)
         y_words = out_1[0].rearrange("p q u -> p (q u)").bitcast(I32)
 
-        def weigh(acc, y, r):
-            nc.scalar.activation(y, acc, SIGMOID, bias=kb_col[:, r : r + 1], scale=ts_col[:, r : r + 1])
+        acc = [psum.tile([P, HALF], F32, name="acc%d" % i, tag="bank%d" % i) for i in range(PACK + AHEAD)]
+        low = slice(0, CHUNK)
+        high = slice(CHUNK, HALF)
 
-        acc = [psum.tile([P, HALF], F32, name="acc%d" % i, tag="bank%d" % i) for i in range(2 * PACK)]
-
-        def out_cols(chunk, r):
-            return acc[PACK * (chunk // 2) + r][:, NMM * (chunk % 2) : NMM * (chunk % 2 + 1)]
-
-        for chunk in range(2):
-            for r in range(PACK):
-                one_pass(out_cols(chunk, r), r, chunk, 0, chunk == 0, False)
+        for r in range(PACK):
+            one_pass(acc[r][:, low], r, 0, q00, True, False)
+        for r in range(PACK):
+            one_pass(acc[r][:, high], r, 0, q01, False, False)
         for r in range(AHEAD):
-            for chunk in (2, 3):
-                one_pass(out_cols(chunk, r), r, chunk, 0, chunk == 2, False)
+            one_pass(acc[PACK + r][:], r, 0, q0b, True, False)
         for h in range(2):
             y = keep.tile([P, PACK, HALF], F32, name="y%d" % h, align_bytes=64)
             span = slice(HALF * h, HALF * (h + 1))
             for r in range(PACK):
-                if h == 1 and r >= AHEAD:
-                    for chunk in (2, 3):
-                        one_pass(out_cols(chunk, r), r, chunk, 0, chunk == 2, False)
-                for chunk in (2 * h + 1, 2 * h):
-                    one_pass(out_cols(chunk, r), r, chunk, 1, False, chunk % 2 == 0)
-                weigh(acc[PACK * h + r][:], y[:, r, :], r)
+                if h == 0:
+                    bank = acc[r]
+                    one_pass(bank[:], r, 1, q1a, False, True)
+                else:
+                    if r < AHEAD:
+                        bank = acc[PACK + r]
+                    else:
+                        bank = psum.tile([P, HALF], F32, name="late%d" % r, tag="bank%d" % (r - AHEAD))
+                        one_pass(bank[:], r, 0, q0b, True, False)
+                    one_pass(bank[:, low], r, 1, q12, False, False)
+                    one_pass(bank[:, high], r, 1, q13, False, True)
+                nc.scalar.activation(y[:, r, :], bank[:], SIGMOID, bias=kb_col[:, r : r + 1], scale=ts_col[:, r : r + 1])
                 if r % 2 == 1:
                     nc.sync.dma_start(y_rows[:, r - 1 : r + 1, span], y[:, r - 1 : r + 1, :])
-            grouped = keep.tile([P, HALF, PACK], BF16, name="yg%d" % h, align_bytes=64)
             if h == 0:
+                grouped = relay.tile([P, HALF, PACK], BF16, name="yg0", align_bytes=64, offset=half_bytes)
                 interleave(nc.vector.tensor_copy, grouped[:], y[:])
             else:
+                grouped = keep.tile([P, HALF, PACK], BF16, name="yg1", align_bytes=64)
                 interleave(nc.vector.tensor_copy, grouped[:, 0:SHARE, :], y[:, :, 0:SHARE])
                 interleave(nc.scalar.copy, grouped[:, SHARE:HALF, :], y[:, :, SHARE:HALF])
-            quantize(y_code, y_scale, HALF * h, HALF, grouped[:])
+            quantize(y_code[:, span], y_scale[:, span], grouped[:])
             nc.sync.dma_start(y_words[:, span], y_code[:, span].bitcast(I32))
         for quad in range(4):
             queue = nc.scalar if quad < 2 else nc.sync

@@ -25,9 +25,7 @@ HALF = NQ // 2
 CHUNK = 128
 LIVE = P - 1
 SROWS = 32
-SHARE = 160
-AHEAD = 2
-SHARE_Q = 160
+LAST = 64
 
 
 def interleave(engine_copy, dst, src):
@@ -44,8 +42,8 @@ def tile_attend_plw_tskb_kernel(tc, qT, k_words, k_scales, ts, kb, offs, out_0, 
         offsets = keep.tile([P, N // 16], U16, name="offsets")
         nc.sync.dma_start(offsets[:], offs)
 
-        half_bytes = 4 * PACK * HALF
-        scale_pool = relay.tile([P, T], U8, name="scale_pool", align_bytes=64, offset=half_bytes - T // 2)
+        chunk_bytes = 4 * PACK * CHUNK
+        scale_pool = relay.tile([P, T], U8, name="scale_pool", align_bytes=64, offset=chunk_bytes // 2)
         ts_pool = keep.tile([P, T], F32, name="ts_pool", align_bytes=64)
         kb_pool = keep.tile([P, T], F32, name="kb_pool", align_bytes=64)
         nc.sync.dma_start(
@@ -54,7 +52,7 @@ def tile_attend_plw_tskb_kernel(tc, qT, k_words, k_scales, ts, kb, offs, out_0, 
         )
         nc.sync.dma_start(ts_pool[LIVE:P, :], ts[0:1, :])
         nc.sync.dma_start(kb_pool[LIVE:P, :], kb[0:1, :])
-        word_pool = keep.tile([P, T], I32, name="word_pool", align_bytes=64)
+        word_pool = relay.tile([P, T], I32, name="word_pool", align_bytes=64, offset=2 * chunk_bytes)
         nc.sync.dma_start(word_pool[:], k_words[0].rearrange("p t b -> p (t b)").bitcast(I32))
         q_rows = qT[0].rearrange("(o p j) w -> o p j w", o=PASSES, j=PACK)
         raw0 = keep.tile([P, PACK, NQ], F32, name="raw0", tag="raw0", align_bytes=64)
@@ -86,10 +84,14 @@ def tile_attend_plw_tskb_kernel(tc, qT, k_words, k_scales, ts, kb, offs, out_0, 
                 scale_dealt[8 * quad : 8 * quad + 8, :].bitcast(I32),
             )
         raw1 = []
-        for h in range(2):
-            half = relay.tile([P, PACK, HALF], F32, name="raw1_%d" % h, align_bytes=64, offset=half_bytes * h)
-            nc.sync.dma_start(half[:], q_rows[1][:, :, HALF * h : HALF * (h + 1)])
-            raw1.append(half)
+
+        def load_chunk(a):
+            raw = relay.tile([P, PACK, CHUNK], F32, name="raw1_%d" % a, align_bytes=64, offset=chunk_bytes * a)
+            nc.sync.dma_start(raw[:], q_rows[1][:, :, CHUNK * a : CHUNK * (a + 1)])
+            raw1.append(raw)
+
+        load_chunk(0)
+        load_chunk(1)
 
         turned = []
         for i, pool in enumerate((ts_pool, kb_pool)):
@@ -102,6 +104,8 @@ def tile_attend_plw_tskb_kernel(tc, qT, k_words, k_scales, ts, kb, offs, out_0, 
 
         word_picked = keep.tile([P, N], U32, name="word_picked", align_bytes=64)
         nc.vector.tensor_copy(word_picked[:], word_pool[:].bitcast(U32).indirect(offsets[:]))
+        load_chunk(2)
+        load_chunk(3)
         halves = word_picked[:].bitcast(U16).rearrange("p (s r o) -> p o s r", r=PACK, o=PASSES)
         k_code = []
         for o in range(PASSES):
@@ -112,17 +116,17 @@ def tile_attend_plw_tskb_kernel(tc, qT, k_words, k_scales, ts, kb, offs, out_0, 
         ts_col = keep.tile([P, PACK], F32, name="ts_col")
         nc.scalar.copy(ts_col[:], turned[0][:, :, LIVE])
 
-        def rounded(src, engine_copy, name, **place):
-            grouped = keep.tile([P, src.shape[2], PACK], BF16, name=name, align_bytes=64, **place)
+        def rounded(src, engine_copy, name, pool=keep, **place):
+            grouped = pool.tile([P, src.shape[2], PACK], BF16, name=name, align_bytes=64, **place)
             interleave(engine_copy, grouped[:], src)
             return grouped[:]
 
         def quantize(codes, scales, grouped):
             nc.vector.quantize_mx(out=codes.bitcast(FP8X4), scales=scales, in_=grouped.rearrange("p w j -> p (w j)"))
 
-        def quantize_q(name, grouped, **place):
+        def quantize_q(name, grouped, pool=keep, **place):
             width = grouped.shape[1]
-            codes = keep.tile([P, width], U32, name=name + "_code", align_bytes=64, **place)
+            codes = pool.tile([P, width], U32, name=name + "_code", align_bytes=64, **place)
             scales = keep.tile([P, width], U8, name=name + "_scale", align_bytes=64)
             quantize(codes[:], scales[:], grouped)
             return codes[:], scales[:]
@@ -137,15 +141,12 @@ def tile_attend_plw_tskb_kernel(tc, qT, k_words, k_scales, ts, kb, offs, out_0, 
         q01 = quantize_q("q01", g01)
         kb_col = keep.tile([P, PACK], F32, name="kb_col", tag="raw0", align_bytes=64)
         nc.scalar.copy(kb_col[:], turned[1][:, :, LIVE])
-        q0b = quantize_q("q0b", g0b)
-        g1a = keep.tile([P, HALF, PACK], BF16, name="g1a", align_bytes=64)
-        interleave(nc.vector.tensor_copy, g1a[:, 0:SHARE_Q, :], raw1[0][:, :, 0:SHARE_Q])
-        interleave(nc.scalar.copy, g1a[:, SHARE_Q:HALF, :], raw1[0][:, :, SHARE_Q:HALF])
-        q1a = quantize_q("q1a", g1a[:])
-        g12 = rounded(cols(raw1[1], 0), nc.vector.tensor_copy, "g12")
-        g13 = rounded(cols(raw1[1], 1), nc.vector.tensor_copy, "g13")
-        q12 = quantize_q("q12", g12)
-        q13 = quantize_q("q13", g13)
+        second = []
+        for a in range(4):
+            second.append(quantize_q("q1%d" % a, rounded(raw1[a][:], nc.vector.tensor_copy, "g1%d" % a)))
+            if a == 0:
+                q0b = quantize_q("q0b", g0b, pool=relay, offset=0)
+        first = [q00, q01] + [(q0b[0][:, piece], q0b[1][:, piece]) for piece in (slice(0, CHUNK), slice(CHUNK, HALF))]
 
         def one_pass(acc, r, o, q, start, stop):
             nc.tensor.matmul_mx(
@@ -163,43 +164,43 @@ def tile_attend_plw_tskb_kernel(tc, qT, k_words, k_scales, ts, kb, offs, out_0, 
         y_rows = out_0.rearrange("(p r) q -> p r q", r=PACK)
         y_words = out_1[0].rearrange("p q u -> p (q u)").bitcast(I32)
 
-        acc = [psum.tile([P, HALF], F32, name="acc%d" % i, tag="bank%d" % i) for i in range(PACK + AHEAD)]
-        low = slice(0, CHUNK)
-        high = slice(CHUNK, HALF)
-
-        for r in range(PACK):
-            one_pass(acc[r][:, low], r, 0, q00, True, False)
-        for r in range(PACK):
-            one_pass(acc[r][:, high], r, 0, q01, False, False)
-        for r in range(AHEAD):
-            one_pass(acc[PACK + r][:], r, 0, q0b, True, False)
-        for h in range(2):
-            y = keep.tile([P, PACK, HALF], F32, name="y%d" % h, align_bytes=64)
-            span = slice(HALF * h, HALF * (h + 1))
+        def first_passes(a):
+            banks = [psum.tile([P, 2, CHUNK], F32, name="acc%d_%d" % (a, i), tag="bank%d" % (2 * (a % 2) + i)) for i in range(2)]
             for r in range(PACK):
-                if h == 0:
-                    bank = acc[r]
-                    one_pass(bank[:], r, 1, q1a, False, True)
-                else:
-                    if r < AHEAD:
-                        bank = acc[PACK + r]
-                    else:
-                        bank = psum.tile([P, HALF], F32, name="late%d" % r, tag="bank%d" % (r - AHEAD))
-                        one_pass(bank[:], r, 0, q0b, True, False)
-                    one_pass(bank[:, low], r, 1, q12, False, False)
-                    one_pass(bank[:, high], r, 1, q13, False, True)
-                nc.scalar.activation(y[:, r, :], bank[:], SIGMOID, bias=kb_col[:, r : r + 1], scale=ts_col[:, r : r + 1])
-                if r % 2 == 1:
-                    nc.sync.dma_start(y_rows[:, r - 1 : r + 1, span], y[:, r - 1 : r + 1, :])
-            if h == 0:
-                grouped = relay.tile([P, HALF, PACK], BF16, name="yg0", align_bytes=64, offset=half_bytes)
-                interleave(nc.vector.tensor_copy, grouped[:], y[:])
-            else:
-                grouped = keep.tile([P, HALF, PACK], BF16, name="yg1", align_bytes=64)
-                interleave(nc.vector.tensor_copy, grouped[:, 0:SHARE, :], y[:, :, 0:SHARE])
-                interleave(nc.scalar.copy, grouped[:, SHARE:HALF, :], y[:, :, SHARE:HALF])
-            quantize(y_code[:, span], y_scale[:, span], grouped[:])
-            nc.sync.dma_start(y_words[:, span], y_code[:, span].bitcast(I32))
+                one_pass(banks[r // 2][:, r % 2, :], r, 0, first[a], r % 2 == 0, False)
+            return banks
+
+        def quantize_y(a, chunks, grouped):
+            span = slice(CHUNK * a, CHUNK * (a + chunks))
+            quantize(y_code[:, span], y_scale[:, span], grouped)
+
+        y = [keep.tile([P, PACK, HALF], F32, name="y%d" % h, align_bytes=64) for h in range(2)]
+        acc = {a: first_passes(a) for a in range(2)}
+        for a in range(4):
+            h = a // 2
+            piece = slice(CHUNK * (a % 2), CHUNK * (a % 2 + 1))
+            span = slice(HALF * h, HALF * (h + 1))
+            if a not in acc:
+                acc[a] = first_passes(a)
+            for r in range(PACK):
+                one_pass(acc[a][r // 2][:, r % 2, :], r, 1, second[a], False, r % 2 == 1)
+            for r in range(PACK):
+                nc.scalar.activation(
+                    y[h][:, r, piece], acc[a][r // 2][:, r % 2, :], SIGMOID, bias=kb_col[:, r : r + 1], scale=ts_col[:, r : r + 1]
+                )
+                if a % 2 == 1 and r % 2 == 1:
+                    nc.sync.dma_start(y_rows[:, r - 1 : r + 1, span], y[h][:, r - 1 : r + 1, :])
+            if a == 1:
+                quantize_y(0, 2, rounded(y[0][:], nc.vector.tensor_copy, "yg0", pool=relay, offset=3 * chunk_bytes))
+            if a == 3:
+                third = rounded(y[1][:, :, 0:CHUNK], nc.vector.tensor_copy, "yg2")
+                grouped = keep.tile([P, CHUNK, PACK], BF16, name="yg3", align_bytes=64)
+                interleave(nc.vector.tensor_copy, grouped[:, 0:LAST, :], y[1][:, :, CHUNK : CHUNK + LAST])
+                interleave(nc.scalar.copy, grouped[:, LAST:CHUNK, :], y[1][:, :, CHUNK + LAST : HALF])
+                quantize_y(2, 1, third)
+                quantize_y(3, 1, grouped[:])
+            if a % 2 == 1:
+                nc.sync.dma_start(y_words[:, span], y_code[:, span].bitcast(I32))
         for quad in range(4):
             queue = nc.scalar if quad < 2 else nc.sync
             queue.dma_start(

@@ -44,13 +44,13 @@ def tile_attend_plw_tskb_kernel(tc, qT, k_words, k_scales, ts, kb, offs, out_0, 
 
         chunk_bytes = 4 * PACK * CHUNK
         scale_pool = relay.tile([P, T], U8, name="scale_pool", align_bytes=64, offset=chunk_bytes // 2)
-        ts_pool = keep.tile([P, T], F32, name="ts_pool", align_bytes=64)
+        ts_pool = keep.tile([P, T + 1], F32, name="ts_pool", align_bytes=64)
         kb_pool = keep.tile([P, T], F32, name="kb_pool", align_bytes=64)
         nc.sync.dma_start(
             scale_pool[0:SROWS, :].bitcast(I32),
             k_scales.rearrange("o f t -> f o t").bitcast(I32),
         )
-        nc.sync.dma_start(ts_pool[LIVE:P, :], ts[0:1, :])
+        nc.sync.dma_start(ts_pool[LIVE:P, 0:T], ts[0:1, :])
         nc.sync.dma_start(kb_pool[LIVE:P, :], kb[0:1, :])
         word_pool = relay.tile([P, T], I32, name="word_pool", align_bytes=64, offset=2 * chunk_bytes)
         nc.sync.dma_start(word_pool[:], k_words[0].rearrange("p t b -> p (t b)").bitcast(I32))
@@ -65,13 +65,13 @@ def tile_attend_plw_tskb_kernel(tc, qT, k_words, k_scales, ts, kb, offs, out_0, 
 
         nc.gpsimd.memset(scale_pool[SROWS : 2 * SROWS, :].bitcast(I32), 0)
         nc.gpsimd.memset(scale_pool[2 * SROWS : P, :].bitcast(I32), 0)
-        nc.vector.memset(ts_pool[0:LIVE, 0 : T - 1], 0.0)
-        nc.vector.memset(ts_pool[0:LIVE, T - 1 : T], 0.0)
-        k_scale = keep.tile([P, PASSES, N], U8, name="k_scale", align_bytes=64)
-        nc.gpsimd.memset(k_scale[:].rearrange("p o n -> p (o n)").bitcast(I32), 0)
+        nc.vector.memset(ts_pool[0:LIVE, :], 0.0)
+        placed = keep.tile([P, PASSES * N + 4], U8, name="placed", align_bytes=64)
+        nc.vector.memset(placed[:].bitcast(I32), 0)
+        k_scale = placed[:, 0 : PASSES * N].rearrange("p (o n) -> p o n", o=PASSES)
+        nc.gpsimd.memset(kb_pool[0:LIVE, :], 0.0)
         ident = keep.tile([P, P], F32, name="ident")
         make_identity(nc, ident[:])
-        nc.gpsimd.memset(kb_pool[0:LIVE, :], 0.0)
 
         scale_dealt = keep.tile([P, N], U8, name="scale_dealt", align_bytes=64)
         nc.vector.tensor_copy(
@@ -96,7 +96,7 @@ def tile_attend_plw_tskb_kernel(tc, qT, k_words, k_scales, ts, kb, offs, out_0, 
         turned = []
         for i, pool in enumerate((ts_pool, kb_pool)):
             picked = keep.tile([P, N], F32, name="picked%d" % i)
-            nc.scalar.activation(picked[:], pool[:].indirect(offsets[:]), COPY)
+            nc.scalar.activation(picked[:], pool[:, 0:T].indirect(offsets[:]), COPY)
             bank = psum.tile([P, PACK, P], F32, name="turned%d" % i, tag="bank%d" % (6 + i))
             for r in range(PACK):
                 nc.tensor.transpose(bank[:, r, :], picked[:, r:N:PACK], ident[:])

@@ -134,7 +134,9 @@ def tile_attend_plw_tskb_kernel(tc, qT, k_words, k_scales, ts, kb, offs, out_0, 
         def cols(raw, a):
             return raw[:, :, CHUNK * a : CHUNK * (a + 1)]
 
-        g00 = rounded(cols(raw0, 0), nc.vector.tensor_copy, "g00")
+        g00 = keep.tile([P, CHUNK, PACK], BF16, name="g00", align_bytes=64)[:]
+        interleave(nc.vector.tensor_copy, g00[:, 0:LAST, :], raw0[:, :, 0:LAST])
+        interleave(nc.scalar.copy, g00[:, LAST:CHUNK, :], raw0[:, :, LAST:CHUNK])
         g01 = rounded(cols(raw0, 1), nc.vector.tensor_copy, "g01")
         g0b = rounded(raw0[:, :, HALF:NQ], nc.scalar.copy, "g0b")
         q00 = quantize_q("q00", g00)

@@ -50,7 +50,7 @@ def tile_attend_plw_tskb_kernel(tc, qT, k_words, k_scales, ts, kb, offs, out_0, 
             scale_pool[0:SROWS, :].bitcast(I32),
             k_scales.rearrange("o f t -> f o t").bitcast(I32),
         )
-        nc.sync.dma_start(ts_pool[LIVE:P, 0:T], ts[0:1, :])
+        nc.scalar.dma_start(ts_pool[LIVE:P, 0:T], ts[0:1, :])
         nc.sync.dma_start(kb_pool[LIVE:P, :], kb[0:1, :])
         word_pool = relay.tile([P, T], I32, name="word_pool", align_bytes=64, offset=2 * chunk_bytes)
         nc.sync.dma_start(word_pool[:], k_words[0].rearrange("p t b -> p (t b)").bitcast(I32))

@@ -43,20 +43,25 @@ def tile_attend_plw_tskb_kernel(tc, qT, k_words, k_scales, ts, kb, offs, out_0, 
         nc.sync.dma_start(offsets[:], offs)
 
         chunk_bytes = 4 * PACK * CHUNK
-        scale_pool = relay.tile([P, T], U8, name="scale_pool", align_bytes=64, offset=chunk_bytes // 2)
+        scale_pool = relay.tile([P, T], U8, name="scale_pool", align_bytes=64, offset=3 * chunk_bytes // 2)
         ts_pool = keep.tile([P, T + 1], F32, name="ts_pool", align_bytes=64)
-        kb_pool = keep.tile([P, T], F32, name="kb_pool", align_bytes=64)
+        kb_pool = keep.tile([P, T], F32, name="kb_pool", tag="kb_pool", align_bytes=64)
         nc.sync.dma_start(
             scale_pool[0:SROWS, :].bitcast(I32),
             k_scales.rearrange("o f t -> f o t").bitcast(I32),
         )
         nc.scalar.dma_start(ts_pool[LIVE:P, 0:T], ts[0:1, :])
         nc.sync.dma_start(kb_pool[LIVE:P, :], kb[0:1, :])
-        word_pool = relay.tile([P, T], I32, name="word_pool", align_bytes=64, offset=2 * chunk_bytes)
+        word_pool = relay.tile([P, T], I32, name="word_pool", align_bytes=64, offset=4 * chunk_bytes)
         nc.sync.dma_start(word_pool[:], k_words[0].rearrange("p t b -> p (t b)").bitcast(I32))
         q_rows = qT[0].rearrange("(o p j) w -> o p j w", o=PASSES, j=PACK)
-        raw0 = keep.tile([P, PACK, NQ], F32, name="raw0", tag="raw0", align_bytes=64)
-        nc.sync.dma_start(raw0[:], q_rows[0])
+
+        def load_q(name, o, first, width, pool=keep, **place):
+            raw = pool.tile([P, PACK, width], F32, name=name, align_bytes=64, **place)
+            nc.sync.dma_start(raw[:], q_rows[o][:, :, first : first + width])
+            return raw
+
+        raw0a = load_q("raw0a", 0, 0, HALF, tag="raw0a")
 
         warm = keep.tile([P, 8], F32, name="warm")
         warm_out = keep.tile([P, 8], F32, name="warm_out")
@@ -69,33 +74,26 @@ def tile_attend_plw_tskb_kernel(tc, qT, k_words, k_scales, ts, kb, offs, out_0, 
         placed = keep.tile([P, PASSES * N + 4], U8, name="placed", align_bytes=64)
         nc.vector.memset(placed[:].bitcast(I32), 0)
         k_scale = placed[:, 0 : PASSES * N].rearrange("p (o n) -> p o n", o=PASSES)
-        nc.gpsimd.memset(kb_pool[0:LIVE, :], 0.0)
         ident = keep.tile([P, P], F32, name="ident")
         make_identity(nc, ident[:])
+        nc.gpsimd.memset(kb_pool[0:LIVE, :], 0.0)
 
         scale_dealt = keep.tile([P, N], U8, name="scale_dealt", align_bytes=64)
         nc.vector.tensor_copy(
             scale_dealt[:].rearrange("p (r s) -> p s r", r=PACK),
             scale_pool[:].indirect(offsets[:]),
         )
-        for quad in range(4):
+        for quad in (0, 2, 1, 3):
             nc.sync.dma_start(
                 k_scale[32 * quad : 32 * quad + 4, :, :].bitcast(I32),
                 scale_dealt[8 * quad : 8 * quad + 8, :].bitcast(I32),
             )
-        raw1 = []
-
-        def load_chunk(a):
-            raw = relay.tile([P, PACK, CHUNK], F32, name="raw1_%d" % a, align_bytes=64, offset=chunk_bytes * a)
-            nc.sync.dma_start(raw[:], q_rows[1][:, :, CHUNK * a : CHUNK * (a + 1)])
-            raw1.append(raw)
-
-        load_chunk(0)
-        load_chunk(1)
+        raw1a = load_q("raw1a", 1, 0, HALF, pool=relay, offset=0)
+        raw0b = load_q("raw0b", 0, HALF, HALF, pool=relay, offset=2 * chunk_bytes)
 
         turned = []
         for i, pool in enumerate((ts_pool, kb_pool)):
-            picked = keep.tile([P, N], F32, name="picked%d" % i)
+            picked = keep.tile([P, N], F32, name="picked%d" % i, tag="picked%d" % i, align_bytes=64)
             nc.scalar.activation(picked[:], pool[:, 0:T].indirect(offsets[:]), COPY)
             bank = psum.tile([P, PACK, P], F32, name="turned%d" % i, tag="bank%d" % (6 + i))
             for r in range(PACK):
@@ -104,8 +102,8 @@ def tile_attend_plw_tskb_kernel(tc, qT, k_words, k_scales, ts, kb, offs, out_0, 
 
         word_picked = keep.tile([P, N], U32, name="word_picked", align_bytes=64)
         nc.vector.tensor_copy(word_picked[:], word_pool[:].bitcast(U32).indirect(offsets[:]))
-        load_chunk(2)
-        load_chunk(3)
+        raw12 = load_q("raw12", 1, 2 * CHUNK, CHUNK, pool=relay, offset=4 * chunk_bytes)
+        raw13 = load_q("raw13", 1, 3 * CHUNK, CHUNK, pool=relay, offset=5 * chunk_bytes)
         halves = word_picked[:].bitcast(U16).rearrange("p (s r o) -> p o s r", r=PACK, o=PASSES)
         k_code = []
         for o in range(PASSES):
@@ -134,22 +132,6 @@ def tile_attend_plw_tskb_kernel(tc, qT, k_words, k_scales, ts, kb, offs, out_0, 
         def cols(raw, a):
             return raw[:, :, CHUNK * a : CHUNK * (a + 1)]
 
-        g00 = keep.tile([P, CHUNK, PACK], BF16, name="g00", align_bytes=64)[:]
-        interleave(nc.vector.tensor_copy, g00[:, 0:LAST, :], raw0[:, :, 0:LAST])
-        interleave(nc.scalar.copy, g00[:, LAST:CHUNK, :], raw0[:, :, LAST:CHUNK])
-        g01 = rounded(cols(raw0, 1), nc.vector.tensor_copy, "g01")
-        g0b = rounded(raw0[:, :, HALF:NQ], nc.scalar.copy, "g0b")
-        q00 = quantize_q("q00", g00)
-        q01 = quantize_q("q01", g01)
-        kb_col = keep.tile([P, PACK], F32, name="kb_col", tag="raw0", align_bytes=64)
-        nc.scalar.copy(kb_col[:], turned[1][:, :, LIVE])
-        second = []
-        for a in range(4):
-            second.append(quantize_q("q1%d" % a, rounded(raw1[a][:], nc.vector.tensor_copy, "g1%d" % a)))
-            if a == 0:
-                q0b = quantize_q("q0b", g0b, pool=relay, offset=0)
-        first = [q00, q01] + [(q0b[0][:, piece], q0b[1][:, piece]) for piece in (slice(0, CHUNK), slice(CHUNK, HALF))]
-
         def one_pass(acc, r, o, q, start, stop):
             nc.tensor.matmul_mx(
                 out=acc,
@@ -165,44 +147,89 @@ def tile_attend_plw_tskb_kernel(tc, qT, k_words, k_scales, ts, kb, offs, out_0, 
         y_scale = keep.tile([P, NQ], U8, name="y_scale", align_bytes=64)
         y_rows = out_0.rearrange("(p r) q -> p r q", r=PACK)
         y_words = out_1[0].rearrange("p q u -> p (q u)").bitcast(I32)
+        y = [keep.tile([P, PACK, HALF], F32, name="y%d" % h, align_bytes=64) for h in range(2)]
 
-        def first_passes(a):
-            banks = [psum.tile([P, 2, CHUNK], F32, name="acc%d_%d" % (a, i), tag="bank%d" % (2 * (a % 2) + i)) for i in range(2)]
-            for r in range(PACK):
-                one_pass(banks[r // 2][:, r % 2, :], r, 0, first[a], r % 2 == 0, False)
-            return banks
+        def weigh(dst, acc, r):
+            nc.scalar.activation(dst, acc, SIGMOID, bias=kb_col[:, r : r + 1], scale=ts_col[:, r : r + 1])
+
+        def store_rows(h, r):
+            nc.sync.dma_start(y_rows[:, r : r + 2, HALF * h : HALF * (h + 1)], y[h][:, r : r + 2, :])
 
         def quantize_y(a, chunks, grouped):
             span = slice(CHUNK * a, CHUNK * (a + chunks))
             quantize(y_code[:, span], y_scale[:, span], grouped)
 
-        y = [keep.tile([P, PACK, HALF], F32, name="y%d" % h, align_bytes=64) for h in range(2)]
-        acc = {a: first_passes(a) for a in range(2)}
-        for a in range(4):
-            h = a // 2
-            piece = slice(CHUNK * (a % 2), CHUNK * (a % 2 + 1))
-            span = slice(HALF * h, HALF * (h + 1))
-            if a not in acc:
-                acc[a] = first_passes(a)
-            for r in range(PACK):
-                one_pass(acc[a][r // 2][:, r % 2, :], r, 1, second[a], False, r % 2 == 1)
-            for r in range(PACK):
-                nc.scalar.activation(
-                    y[h][:, r, piece], acc[a][r // 2][:, r % 2, :], SIGMOID, bias=kb_col[:, r : r + 1], scale=ts_col[:, r : r + 1]
-                )
-                if a % 2 == 1 and r % 2 == 1:
-                    nc.sync.dma_start(y_rows[:, r - 1 : r + 1, span], y[h][:, r - 1 : r + 1, :])
-            if a == 1:
-                quantize_y(0, 2, rounded(y[0][:], nc.vector.tensor_copy, "yg0", pool=relay, offset=3 * chunk_bytes))
-            if a == 3:
-                third = rounded(y[1][:, :, 0:CHUNK], nc.vector.tensor_copy, "yg2")
-                grouped = keep.tile([P, CHUNK, PACK], BF16, name="yg3", align_bytes=64)
-                interleave(nc.vector.tensor_copy, grouped[:, 0:LAST, :], y[1][:, :, CHUNK : CHUNK + LAST])
-                interleave(nc.scalar.copy, grouped[:, LAST:CHUNK, :], y[1][:, :, CHUNK + LAST : HALF])
-                quantize_y(2, 1, third)
-                quantize_y(3, 1, grouped[:])
-            if a % 2 == 1:
-                nc.sync.dma_start(y_words[:, span], y_code[:, span].bitcast(I32))
+        g00 = rounded(cols(raw0a, 0), nc.scalar.copy, "g00", tag="kb_pool")
+        g01 = rounded(cols(raw0a, 1), nc.vector.tensor_copy, "g01")
+        shared = keep.tile([P, 2, CHUNK], U32, name="q0a_code", tag="picked1", align_bytes=64)
+        early = []
+        for a, grouped in enumerate((g00, g01)):
+            scales = keep.tile([P, CHUNK], U8, name="q0%d_scale" % a, align_bytes=64)
+            quantize(shared[:, a, :], scales[:], grouped)
+            early.append((shared[:, a, :], scales[:]))
+        q00, q01 = early
+        kb_col = keep.tile([P, PACK], F32, name="kb_col", tag="raw0a", align_bytes=64)
+        nc.scalar.copy(kb_col[:], turned[1][:, :, LIVE])
+        lead = [psum.tile([P, 2, CHUNK], F32, name="lead%d" % a, tag="bank%d" % a) for a in range(2)]
+        wide = [psum.tile([P, 2, CHUNK], F32, name="wide%d" % i, tag="bank%d" % (2 + i)) for i in range(2)]
+
+        def half_passes(o, a, q, rows):
+            for r in rows:
+                if r < 2:
+                    one_pass(lead[a][:, r, :], r, o, q, o == 0 and r == 0, o == 1 and r == 1)
+                else:
+                    one_pass(wide[r - 2][:, a, :], r, o, q, o == 0 and a == 0, o == 1 and a == 1)
+
+        for a, q in enumerate((q00, q01)):
+            half_passes(0, a, q, range(PACK))
+        g10 = rounded(cols(raw1a, 0), nc.vector.tensor_copy, "g10", tag="kb_pool")
+        g11 = rounded(cols(raw1a, 1), nc.scalar.copy, "g11", tag="g11")
+        q10 = quantize_q("q10", g10)
+        q11 = quantize_q("q11", g11)
+        for rows in ((0, 1), (2, 3)):
+            for a, q in enumerate((q10, q11)):
+                half_passes(1, a, q, rows)
+        for a in range(2):
+            for r in range(2):
+                weigh(y[0][:, r, CHUNK * a : CHUNK * (a + 1)], lead[a][:, r, :], r)
+        store_rows(0, 0)
+        for r in range(2, PACK):
+            weigh(y[0][:, r, :], wide[r - 2][:].rearrange("p a c -> p (a c)"), r)
+        store_rows(0, 2)
+
+        g0b = keep.tile([P, HALF, PACK], BF16, name="g0b", tag="g11", align_bytes=64)
+        g02, g03 = g0b[:, 0:CHUNK, :], g0b[:, CHUNK:HALF, :]
+        interleave(nc.vector.tensor_copy, g02, cols(raw0b, 0))
+        interleave(nc.vector.tensor_copy, g03, cols(raw0b, 1))
+        q02 = quantize_q("q02", g02)
+        q03 = quantize_q("q03", g03)
+        pairs = [psum.tile([P, 2, CHUNK], F32, name="pair%d" % i, tag="bank%d" % (4 + i)) for i in range(2)]
+        single = [psum.tile([P, CHUNK], F32, name="single%d" % r, tag="bank%d" % ((6 + r) % 8)) for r in range(PACK)]
+        for r in range(PACK):
+            one_pass(pairs[r // 2][:, r % 2, :], r, 0, q02, r % 2 == 0, False)
+        for r in range(PACK):
+            one_pass(single[r][:], r, 0, q03, True, False)
+        q12 = quantize_q("q12", rounded(raw12[:], nc.vector.tensor_copy, "g12"))
+        q13 = quantize_q("q13", rounded(raw13[:], nc.vector.tensor_copy, "g13"))
+        yg0 = rounded(y[0][:], nc.vector.tensor_copy, "yg0", pool=relay, offset=5 * chunk_bytes)
+        for r in range(PACK):
+            one_pass(pairs[r // 2][:, r % 2, :], r, 1, q12, False, r % 2 == 1)
+        for r in range(PACK):
+            one_pass(single[r][:], r, 1, q13, False, True)
+        for r in range(PACK):
+            weigh(y[1][:, r, 0:CHUNK], pairs[r // 2][:, r % 2, :], r)
+        quantize_y(0, 2, yg0)
+        nc.sync.dma_start(y_words[:, 0:HALF], y_code[:, 0:HALF].bitcast(I32))
+        for r in range(PACK):
+            weigh(y[1][:, r, CHUNK:HALF], single[r][:], r)
+            if r % 2 == 1:
+                store_rows(1, r - 1)
+        quantize_y(2, 1, rounded(y[1][:, :, 0:CHUNK], nc.vector.tensor_copy, "yg2"))
+        grouped = keep.tile([P, CHUNK, PACK], BF16, name="yg3", align_bytes=64)
+        interleave(nc.vector.tensor_copy, grouped[:, 0:LAST, :], y[1][:, :, CHUNK : CHUNK + LAST])
+        interleave(nc.scalar.copy, grouped[:, LAST:CHUNK, :], y[1][:, :, CHUNK + LAST : HALF])
+        quantize_y(3, 1, grouped[:])
+        nc.sync.dma_start(y_words[:, HALF:NQ], y_code[:, HALF:NQ].bitcast(I32))
         for quad in range(4):
             queue = nc.scalar if quad < 2 else nc.sync
             queue.dma_start(

@@ -25,7 +25,9 @@ HALF = NQ // 2
 CHUNK = 128
 LIVE = P - 1
 SROWS = 32
+LINE = 256
 LAST = 64
+PIECE = 192
 
 
 def interleave(engine_copy, dst, src):
@@ -43,21 +45,21 @@ def tile_attend_plw_tskb_kernel(tc, qT, k_words, k_scales, ts, kb, offs, out_0, 
         nc.sync.dma_start(offsets[:], offs)
 
         chunk_bytes = 4 * PACK * CHUNK
-        scale_pool = relay.tile([P, T], U8, name="scale_pool", align_bytes=64, offset=3 * chunk_bytes // 2)
-        ts_pool = keep.tile([P, T + 1], F32, name="ts_pool", align_bytes=64)
-        kb_pool = keep.tile([P, T], F32, name="kb_pool", tag="kb_pool", align_bytes=64)
+        scale_pool = relay.tile([P, T], U8, name="scale_pool", align_bytes=LINE, offset=chunk_bytes)
+        ts_pool = keep.tile([P, T + 1], F32, name="ts_pool", align_bytes=LINE)
+        kb_pool = keep.tile([P, T], F32, name="kb_pool", tag="kb_pool", align_bytes=LINE)
         nc.sync.dma_start(
             scale_pool[0:SROWS, :].bitcast(I32),
             k_scales.rearrange("o f t -> f o t").bitcast(I32),
         )
         nc.scalar.dma_start(ts_pool[LIVE:P, 0:T], ts[0:1, :])
         nc.sync.dma_start(kb_pool[LIVE:P, :], kb[0:1, :])
-        word_pool = relay.tile([P, T], I32, name="word_pool", align_bytes=64, offset=4 * chunk_bytes)
+        word_pool = relay.tile([P, T], I32, name="word_pool", align_bytes=LINE, offset=3 * chunk_bytes)
         nc.sync.dma_start(word_pool[:], k_words[0].rearrange("p t b -> p (t b)").bitcast(I32))
         q_rows = qT[0].rearrange("(o p j) w -> o p j w", o=PASSES, j=PACK)
 
         def load_q(name, o, first, width, pool=keep, **place):
-            raw = pool.tile([P, PACK, width], F32, name=name, align_bytes=64, **place)
+            raw = pool.tile([P, PACK, width], F32, name=name, align_bytes=LINE, **place)
             nc.sync.dma_start(raw[:], q_rows[o][:, :, first : first + width])
             return raw
 
@@ -71,14 +73,14 @@ def tile_attend_plw_tskb_kernel(tc, qT, k_words, k_scales, ts, kb, offs, out_0, 
         nc.gpsimd.memset(scale_pool[SROWS : 2 * SROWS, :].bitcast(I32), 0)
         nc.gpsimd.memset(scale_pool[2 * SROWS : P, :].bitcast(I32), 0)
         nc.vector.memset(ts_pool[0:LIVE, :], 0.0)
-        placed = keep.tile([P, PASSES * N + 4], U8, name="placed", align_bytes=64)
+        placed = keep.tile([P, PASSES * N + 4], U8, name="placed", align_bytes=LINE)
         nc.vector.memset(placed[:].bitcast(I32), 0)
         k_scale = placed[:, 0 : PASSES * N].rearrange("p (o n) -> p o n", o=PASSES)
         ident = keep.tile([P, P], F32, name="ident")
         make_identity(nc, ident[:])
         nc.gpsimd.memset(kb_pool[0:LIVE, :], 0.0)
 
-        scale_dealt = keep.tile([P, N], U8, name="scale_dealt", align_bytes=64)
+        scale_dealt = keep.tile([P, N], U8, name="scale_dealt", align_bytes=LINE)
         nc.vector.tensor_copy(
             scale_dealt[:].rearrange("p (r s) -> p s r", r=PACK),
             scale_pool[:].indirect(offsets[:]),
@@ -88,26 +90,26 @@ def tile_attend_plw_tskb_kernel(tc, qT, k_words, k_scales, ts, kb, offs, out_0, 
                 k_scale[32 * quad : 32 * quad + 4, :, :].bitcast(I32),
                 scale_dealt[8 * quad : 8 * quad + 8, :].bitcast(I32),
             )
-        raw1a = load_q("raw1a", 1, 0, HALF, pool=relay, offset=0)
-        raw0b = load_q("raw0b", 0, HALF, HALF, pool=relay, offset=2 * chunk_bytes)
+        raw1a = load_q("raw1a", 1, 0, PIECE, pool=relay, offset=0)
+        raw1b = load_q("raw1b", 1, PIECE, PIECE, pool=relay, offset=3 * chunk_bytes // 2)
 
         turned = []
         for i, pool in enumerate((ts_pool, kb_pool)):
-            picked = keep.tile([P, N], F32, name="picked%d" % i, tag="picked%d" % i, align_bytes=64)
+            picked = keep.tile([P, N], F32, name="picked%d" % i, tag="picked%d" % i, align_bytes=LINE)
             nc.scalar.activation(picked[:], pool[:, 0:T].indirect(offsets[:]), COPY)
             bank = psum.tile([P, PACK, P], F32, name="turned%d" % i, tag="bank%d" % (6 + i))
             for r in range(PACK):
                 nc.tensor.transpose(bank[:, r, :], picked[:, r:N:PACK], ident[:])
             turned.append(bank)
 
-        word_picked = keep.tile([P, N], U32, name="word_picked", align_bytes=64)
+        word_picked = keep.tile([P, N], U32, name="word_picked", align_bytes=LINE)
         nc.vector.tensor_copy(word_picked[:], word_pool[:].bitcast(U32).indirect(offsets[:]))
-        raw12 = load_q("raw12", 1, 2 * CHUNK, CHUNK, pool=relay, offset=4 * chunk_bytes)
+        raw0b = load_q("raw0b", 0, HALF, HALF, pool=relay, offset=3 * chunk_bytes)
         raw13 = load_q("raw13", 1, 3 * CHUNK, CHUNK, pool=relay, offset=5 * chunk_bytes)
         halves = word_picked[:].bitcast(U16).rearrange("p (s r o) -> p o s r", r=PACK, o=PASSES)
         k_code = []
         for o in range(PASSES):
-            parted = keep.tile([P, 2 * N], U8, name="k_code%d" % o, align_bytes=64)
+            parted = keep.tile([P, 2 * N], U8, name="k_code%d" % o, align_bytes=LINE)
             nc.vector.tensor_copy(parted[:].bitcast(U16).rearrange("p (r s) -> p s r", r=PACK), halves[:, o, :, :])
             k_code.append(parted)
 
@@ -115,7 +117,7 @@ def tile_attend_plw_tskb_kernel(tc, qT, k_words, k_scales, ts, kb, offs, out_0, 
         nc.scalar.copy(ts_col[:], turned[0][:, :, LIVE])
 
         def rounded(src, engine_copy, name, pool=keep, **place):
-            grouped = pool.tile([P, src.shape[2], PACK], BF16, name=name, align_bytes=64, **place)
+            grouped = pool.tile([P, src.shape[2], PACK], BF16, name=name, align_bytes=LINE, **place)
             interleave(engine_copy, grouped[:], src)
             return grouped[:]
 
@@ -124,8 +126,8 @@ def tile_attend_plw_tskb_kernel(tc, qT, k_words, k_scales, ts, kb, offs, out_0, 
 
         def quantize_q(name, grouped, pool=keep, **place):
             width = grouped.shape[1]
-            codes = pool.tile([P, width], U32, name=name + "_code", align_bytes=64, **place)
-            scales = keep.tile([P, width], U8, name=name + "_scale", align_bytes=64)
+            codes = pool.tile([P, width], U32, name=name + "_code", align_bytes=LINE, **place)
+            scales = keep.tile([P, width], U8, name=name + "_scale", align_bytes=LINE)
             quantize(codes[:], scales[:], grouped)
             return codes[:], scales[:]
 
@@ -143,11 +145,11 @@ def tile_attend_plw_tskb_kernel(tc, qT, k_words, k_scales, ts, kb, offs, out_0, 
                 stop=stop,
             )
 
-        y_code = keep.tile([P, NQ], U32, name="y_code", align_bytes=64)
-        y_scale = keep.tile([P, NQ], U8, name="y_scale", align_bytes=64)
+        y_code = keep.tile([P, NQ], U32, name="y_code", align_bytes=LINE)
+        y_scale = keep.tile([P, NQ], U8, name="y_scale", align_bytes=LINE)
         y_rows = out_0.rearrange("(p r) q -> p r q", r=PACK)
         y_words = out_1[0].rearrange("p q u -> p (q u)").bitcast(I32)
-        y = [keep.tile([P, PACK, HALF], F32, name="y%d" % h, align_bytes=64) for h in range(2)]
+        y = [keep.tile([P, PACK, HALF], F32, name="y%d" % h, align_bytes=LINE) for h in range(2)]
 
         def weigh(dst, acc, r):
             nc.scalar.activation(dst, acc, SIGMOID, bias=kb_col[:, r : r + 1], scale=ts_col[:, r : r + 1])
@@ -161,63 +163,65 @@ def tile_attend_plw_tskb_kernel(tc, qT, k_words, k_scales, ts, kb, offs, out_0, 
 
         g00 = rounded(cols(raw0a, 0), nc.scalar.copy, "g00", tag="kb_pool")
         g01 = rounded(cols(raw0a, 1), nc.vector.tensor_copy, "g01")
-        shared = keep.tile([P, 2, CHUNK], U32, name="q0a_code", tag="picked1", align_bytes=64)
+        shared = keep.tile([P, 2, CHUNK], U32, name="q0a_code", tag="picked1", align_bytes=LINE)
         early = []
         for a, grouped in enumerate((g00, g01)):
-            scales = keep.tile([P, CHUNK], U8, name="q0%d_scale" % a, align_bytes=64)
+            scales = keep.tile([P, CHUNK], U8, name="q0%d_scale" % a, align_bytes=LINE)
             quantize(shared[:, a, :], scales[:], grouped)
             early.append((shared[:, a, :], scales[:]))
         q00, q01 = early
-        kb_col = keep.tile([P, PACK], F32, name="kb_col", tag="raw0a", align_bytes=64)
+        kb_col = keep.tile([P, PACK], F32, name="kb_col", tag="raw0a", align_bytes=LINE)
         nc.scalar.copy(kb_col[:], turned[1][:, :, LIVE])
-        lead = [psum.tile([P, 2, CHUNK], F32, name="lead%d" % a, tag="bank%d" % a) for a in range(2)]
-        wide = [psum.tile([P, 2, CHUNK], F32, name="wide%d" % i, tag="bank%d" % (2 + i)) for i in range(2)]
+        pairs = [
+            [psum.tile([P, 2, CHUNK], F32, name="pair%d_%d" % (a, i), tag="bank%d" % (2 * a + i)) for i in range(2)]
+            for a in range(2)
+        ]
 
-        def half_passes(o, a, q, rows):
-            for r in rows:
-                if r < 2:
-                    one_pass(lead[a][:, r, :], r, o, q, o == 0 and r == 0, o == 1 and r == 1)
-                else:
-                    one_pass(wide[r - 2][:, a, :], r, o, q, o == 0 and a == 0, o == 1 and a == 1)
+        def pair_passes(a, o, q):
+            for r in range(PACK):
+                one_pass(pairs[a][r // 2][:, r % 2, :], r, o, q, o == 0 and r % 2 == 0, o == 1 and r % 2 == 1)
 
-        for a, q in enumerate((q00, q01)):
-            half_passes(0, a, q, range(PACK))
+        def pair_weights(a):
+            for r in range(PACK):
+                weigh(y[0][:, r, CHUNK * a : CHUNK * (a + 1)], pairs[a][r // 2][:, r % 2, :], r)
+                if a == 1 and r % 2 == 1:
+                    store_rows(0, r - 1)
+
+        pair_passes(0, 0, q00)
+        pair_passes(1, 0, q01)
         g10 = rounded(cols(raw1a, 0), nc.vector.tensor_copy, "g10", tag="kb_pool")
-        g11 = rounded(cols(raw1a, 1), nc.scalar.copy, "g11", tag="g11")
-        q10 = quantize_q("q10", g10)
-        q11 = quantize_q("q11", g11)
-        for rows in ((0, 1), (2, 3)):
-            for a, q in enumerate((q10, q11)):
-                half_passes(1, a, q, rows)
-        for a in range(2):
-            for r in range(2):
-                weigh(y[0][:, r, CHUNK * a : CHUNK * (a + 1)], lead[a][:, r, :], r)
-        store_rows(0, 0)
-        for r in range(2, PACK):
-            weigh(y[0][:, r, :], wide[r - 2][:].rearrange("p a c -> p (a c)"), r)
-        store_rows(0, 2)
+        g11 = keep.tile([P, CHUNK, PACK], BF16, name="g11", align_bytes=LINE)
+        interleave(nc.scalar.copy, g11[:, 0 : PIECE - CHUNK, :], raw1a[:, :, CHUNK:PIECE])
+        pair_passes(0, 1, quantize_q("q10", g10))
+        pair_weights(0)
+        interleave(nc.vector.tensor_copy, g11[:, PIECE - CHUNK : CHUNK, :], raw1b[:, :, 0 : HALF - PIECE])
+        g12 = rounded(raw1b[:, :, HALF - PIECE : PIECE], nc.vector.tensor_copy, "g12", tag="g12")
+        pair_passes(1, 1, quantize_q("q11", g11[:]))
+        q12 = quantize_q("q12", g12)
+        pair_weights(1)
 
-        g0b = keep.tile([P, HALF, PACK], BF16, name="g0b", tag="g11", align_bytes=64)
+        alone = [psum.tile([P, CHUNK], F32, name="alone%d" % r, tag="bank%d" % (4 + r)) for r in range(2)]
+        pair = psum.tile([P, 2, CHUNK], F32, name="pair", tag="bank6")
+        third = [alone[0][:], alone[1][:], pair[:, 0, :], pair[:, 1, :]]
+        single = [psum.tile([P, CHUNK], F32, name="single%d" % r, tag="bank%d" % ((7 + r) % 8)) for r in range(PACK)]
+        for r in range(PACK):
+            one_pass(third[r], r, 1, q12, r != 3, False)
+        g0b = keep.tile([P, HALF, PACK], BF16, name="g0b", tag="g12", align_bytes=LINE)
         g02, g03 = g0b[:, 0:CHUNK, :], g0b[:, CHUNK:HALF, :]
         interleave(nc.vector.tensor_copy, g02, cols(raw0b, 0))
         interleave(nc.vector.tensor_copy, g03, cols(raw0b, 1))
         q02 = quantize_q("q02", g02)
         q03 = quantize_q("q03", g03)
-        pairs = [psum.tile([P, 2, CHUNK], F32, name="pair%d" % i, tag="bank%d" % (4 + i)) for i in range(2)]
-        single = [psum.tile([P, CHUNK], F32, name="single%d" % r, tag="bank%d" % ((6 + r) % 8)) for r in range(PACK)]
         for r in range(PACK):
-            one_pass(pairs[r // 2][:, r % 2, :], r, 0, q02, r % 2 == 0, False)
+            one_pass(third[r], r, 0, q02, False, r != 2)
         for r in range(PACK):
             one_pass(single[r][:], r, 0, q03, True, False)
-        q12 = quantize_q("q12", rounded(raw12[:], nc.vector.tensor_copy, "g12"))
         q13 = quantize_q("q13", rounded(raw13[:], nc.vector.tensor_copy, "g13"))
         yg0 = rounded(y[0][:], nc.vector.tensor_copy, "yg0", pool=relay, offset=5 * chunk_bytes)
         for r in range(PACK):
-            one_pass(pairs[r // 2][:, r % 2, :], r, 1, q12, False, r % 2 == 1)
-        for r in range(PACK):
             one_pass(single[r][:], r, 1, q13, False, True)
         for r in range(PACK):
-            weigh(y[1][:, r, 0:CHUNK], pairs[r // 2][:, r % 2, :], r)
+            weigh(y[1][:, r, 0:CHUNK], third[r], r)
         quantize_y(0, 2, yg0)
         nc.sync.dma_start(y_words[:, 0:HALF], y_code[:, 0:HALF].bitcast(I32))
         for r in range(PACK):
@@ -225,7 +229,7 @@ def tile_attend_plw_tskb_kernel(tc, qT, k_words, k_scales, ts, kb, offs, out_0, 
             if r % 2 == 1:
                 store_rows(1, r - 1)
         quantize_y(2, 1, rounded(y[1][:, :, 0:CHUNK], nc.vector.tensor_copy, "yg2"))
-        grouped = keep.tile([P, CHUNK, PACK], BF16, name="yg3", align_bytes=64)
+        grouped = keep.tile([P, CHUNK, PACK], BF16, name="yg3", align_bytes=LINE)
         interleave(nc.vector.tensor_copy, grouped[:, 0:LAST, :], y[1][:, :, CHUNK : CHUNK + LAST])
         interleave(nc.scalar.copy, grouped[:, LAST:CHUNK, :], y[1][:, :, CHUNK + LAST : HALF])
         quantize_y(3, 1, grouped[:])

@@ -223,17 +223,17 @@ def tile_attend_plw_tskb_kernel(tc, qT, k_words, k_scales, ts, kb, offs, out_0, 
         for r in range(PACK):
             weigh(y[1][:, r, 0:CHUNK], third[r], r)
         quantize_y(0, 2, yg0)
-        nc.sync.dma_start(y_words[:, 0:HALF], y_code[:, 0:HALF].bitcast(I32))
         for r in range(PACK):
             weigh(y[1][:, r, CHUNK:HALF], single[r][:], r)
             if r % 2 == 1:
                 store_rows(1, r - 1)
         quantize_y(2, 1, rounded(y[1][:, :, 0:CHUNK], nc.vector.tensor_copy, "yg2"))
+        nc.sync.dma_start(y_words[:, 0 : 3 * CHUNK], y_code[:, 0 : 3 * CHUNK].bitcast(I32))
         grouped = keep.tile([P, CHUNK, PACK], BF16, name="yg3", align_bytes=LINE)
         interleave(nc.vector.tensor_copy, grouped[:, 0:LAST, :], y[1][:, :, CHUNK : CHUNK + LAST])
         interleave(nc.scalar.copy, grouped[:, LAST:CHUNK, :], y[1][:, :, CHUNK + LAST : HALF])
         quantize_y(3, 1, grouped[:])
-        nc.sync.dma_start(y_words[:, HALF:NQ], y_code[:, HALF:NQ].bitcast(I32))
+        nc.sync.dma_start(y_words[:, 3 * CHUNK : NQ], y_code[:, 3 * CHUNK : NQ].bitcast(I32))
         for quad in range(4):
             queue = nc.scalar if quad < 2 else nc.sync
             queue.dma_start(

from contextlib import ExitStack

import concourse.mybir as mybir
from concourse.masks import make_identity

N, T, D, NQ = 512, 2048, 1024, 512
FLOPS = 2 * N * D * NQ
BYTES = 4 * D * NQ + 128 * T * 4 + 32 * T + 2 * 4 * T + 128 * 32 * 2 + 4 * N * NQ + N * NQ + 16 * NQ

F32 = mybir.dt.float32
BF16 = mybir.dt.bfloat16
I32 = mybir.dt.int32
U32 = mybir.dt.uint32
U16 = mybir.dt.uint16
U8 = mybir.dt.uint8
FP8X4 = mybir.dt.float8_e4m3fn_x4
FP4X4 = mybir.dt.float4_e2m1fn_x4
SIGMOID = mybir.ActivationFunctionType.Sigmoid
COPY = mybir.ActivationFunctionType.Copy

P = 128
PACK = 4
PASSES = D // (P * PACK)
HALF = NQ // 2
CHUNK = 128
LIVE = P - 1
SROWS = 32
LINE = 256
LAST = 64
PIECE = 192


def interleave(engine_copy, dst, src):
    engine_copy(dst.rearrange("p (c i) t -> p c t i", i=4), src.rearrange("p t (c i) -> p c t i", i=4))


def tile_attend_plw_tskb_kernel(tc, qT, k_words, k_scales, ts, kb, offs, out_0, out_1, out_2):
    nc = tc.nc
    with ExitStack() as ctx:
        keep = ctx.enter_context(tc.tile_pool(name="keep", bufs=1))
        relay = ctx.enter_context(tc.tile_pool(name="relay", bufs=1))
        psum = ctx.enter_context(tc.psum_pool(name="psum", bufs=1))

        offsets = keep.tile([P, N // 16], U16, name="offsets")
        nc.sync.dma_start(offsets[:], offs)

        chunk_bytes = 4 * PACK * CHUNK
        scale_pool = relay.tile([P, T], U8, name="scale_pool", align_bytes=LINE, offset=chunk_bytes)
        ts_pool = keep.tile([P, T + 1], F32, name="ts_pool", align_bytes=LINE)
        kb_pool = keep.tile([P, T], F32, name="kb_pool", tag="kb_pool", align_bytes=LINE)
        nc.sync.dma_start(
            scale_pool[0:SROWS, :].bitcast(I32),
            k_scales.rearrange("o f t -> f o t").bitcast(I32),
        )
        nc.scalar.dma_start(ts_pool[LIVE:P, 0:T], ts[0:1, :])
        nc.sync.dma_start(kb_pool[LIVE:P, :], kb[0:1, :])
        word_pool = relay.tile([P, T], I32, name="word_pool", align_bytes=LINE, offset=3 * chunk_bytes)
        nc.sync.dma_start(word_pool[:], k_words[0].rearrange("p t b -> p (t b)").bitcast(I32))
        q_rows = qT[0].rearrange("(o p j) w -> o p j w", o=PASSES, j=PACK)

        def load_q(name, o, first, width, pool=keep, **place):
            raw = pool.tile([P, PACK, width], F32, name=name, align_bytes=LINE, **place)
            nc.sync.dma_start(raw[:], q_rows[o][:, :, first : first + width])
            return raw

        raw0a = load_q("raw0a", 0, 0, HALF, tag="raw0a")

        warm = keep.tile([P, 8], F32, name="warm")
        warm_out = keep.tile([P, 8], F32, name="warm_out")
        nc.gpsimd.memset(warm[:], 0.0)
        nc.scalar.activation(warm_out[:], warm[:], SIGMOID)

        nc.gpsimd.memset(scale_pool[SROWS : 2 * SROWS, :].bitcast(I32), 0)
        nc.gpsimd.memset(scale_pool[2 * SROWS : P, :].bitcast(I32), 0)
        nc.vector.memset(ts_pool[0:LIVE, :], 0.0)
        placed = keep.tile([P, PASSES * N + 4], U8, name="placed", align_bytes=LINE)
        nc.vector.memset(placed[:].bitcast(I32), 0)
        k_scale = placed[:, 0 : PASSES * N].rearrange("p (o n) -> p o n", o=PASSES)
        ident = keep.tile([P, P], F32, name="ident")
        make_identity(nc, ident[:])
        nc.gpsimd.memset(kb_pool[0:LIVE, :], 0.0)

        scale_dealt = keep.tile([P, N], U8, name="scale_dealt", align_bytes=LINE)
        nc.vector.tensor_copy(
            scale_dealt[:].rearrange("p (r s) -> p s r", r=PACK),
            scale_pool[:].indirect(offsets[:]),
        )
        for quad in (0, 2, 1, 3):
            nc.sync.dma_start(
                k_scale[32 * quad : 32 * quad + 4, :, :].bitcast(I32),
                scale_dealt[8 * quad : 8 * quad + 8, :].bitcast(I32),
            )
        raw1a = load_q("raw1a", 1, 0, PIECE, pool=relay, offset=0)
        raw1b = load_q("raw1b", 1, PIECE, PIECE, pool=relay, offset=3 * chunk_bytes // 2)

        turned = []
        for i, pool in enumerate((ts_pool, kb_pool)):
            picked = keep.tile([P, N], F32, name="picked%d" % i, tag="picked%d" % i, align_bytes=LINE)
            nc.scalar.activation(picked[:], pool[:, 0:T].indirect(offsets[:]), COPY)
            bank = psum.tile([P, PACK, P], F32, name="turned%d" % i, tag="bank%d" % (6 + i))
            for r in range(PACK):
                nc.tensor.transpose(bank[:, r, :], picked[:, r:N:PACK], ident[:])
            turned.append(bank)

        word_picked = keep.tile([P, N], U32, name="word_picked", align_bytes=LINE)
        nc.vector.tensor_copy(word_picked[:], word_pool[:].bitcast(U32).indirect(offsets[:]))
        raw0b = load_q("raw0b", 0, HALF, HALF, pool=relay, offset=3 * chunk_bytes)
        raw13 = load_q("raw13", 1, 3 * CHUNK, CHUNK, pool=relay, offset=5 * chunk_bytes)
        halves = word_picked[:].bitcast(U16).rearrange("p (s r o) -> p o s r", r=PACK, o=PASSES)
        k_code = []
        for o in range(PASSES):
            parted = keep.tile([P, 2 * N], U8, name="k_code%d" % o, align_bytes=LINE)
            nc.vector.tensor_copy(parted[:].bitcast(U16).rearrange("p (r s) -> p s r", r=PACK), halves[:, o, :, :])
            k_code.append(parted)

        ts_col = keep.tile([P, PACK], F32, name="ts_col")
        nc.scalar.copy(ts_col[:], turned[0][:, :, LIVE])

        def rounded(src, engine_copy, name, pool=keep, **place):
            grouped = pool.tile([P, src.shape[2], PACK], BF16, name=name, align_bytes=LINE, **place)
            interleave(engine_copy, grouped[:], src)
            return grouped[:]

        def quantize(codes, scales, grouped):
            nc.vector.quantize_mx(out=codes.bitcast(FP8X4), scales=scales, in_=grouped.rearrange("p w j -> p (w j)"))

        def quantize_q(name, grouped, pool=keep, **place):
            width = grouped.shape[1]
            codes = pool.tile([P, width], U32, name=name + "_code", align_bytes=LINE, **place)
            scales = keep.tile([P, width], U8, name=name + "_scale", align_bytes=LINE)
            quantize(codes[:], scales[:], grouped)
            return codes[:], scales[:]

        def cols(raw, a):
            return raw[:, :, CHUNK * a : CHUNK * (a + 1)]

        def one_pass(acc, r, o, q, start, stop):
            nc.tensor.matmul_mx(
                out=acc,
                lhsT=k_code[o][:, 2 * P * r : 2 * P * (r + 1)].bitcast(FP4X4),
                lhsT_scale=k_scale[:, o, P * r : P * (r + 1)],
                rhs=q[0].bitcast(FP8X4),
                rhs_scale=q[1],
                start=start,
                stop=stop,
            )

        y_code = keep.tile([P, NQ], U32, name="y_code", align_bytes=LINE)
        y_scale = keep.tile([P, NQ], U8, name="y_scale", align_bytes=LINE)
        y_rows = out_0.rearrange("(p r) q -> p r q", r=PACK)
        y_words = out_1[0].rearrange("p q u -> p (q u)").bitcast(I32)
        y = [keep.tile([P, PACK, HALF], F32, name="y%d" % h, align_bytes=LINE) for h in range(2)]

        def weigh(dst, acc, r):
            nc.scalar.activation(dst, acc, SIGMOID, bias=kb_col[:, r : r + 1], scale=ts_col[:, r : r + 1])

        def store_rows(h, r):
            nc.sync.dma_start(y_rows[:, r : r + 2, HALF * h : HALF * (h + 1)], y[h][:, r : r + 2, :])

        def quantize_y(a, chunks, grouped):
            span = slice(CHUNK * a, CHUNK * (a + chunks))
            quantize(y_code[:, span], y_scale[:, span], grouped)

        g00 = rounded(cols(raw0a, 0), nc.scalar.copy, "g00", tag="kb_pool")
        g01 = rounded(cols(raw0a, 1), nc.vector.tensor_copy, "g01")
        shared = keep.tile([P, 2, CHUNK], U32, name="q0a_code", tag="picked1", align_bytes=LINE)
        early = []
        for a, grouped in enumerate((g00, g01)):
            scales = keep.tile([P, CHUNK], U8, name="q0%d_scale" % a, align_bytes=LINE)
            quantize(shared[:, a, :], scales[:], grouped)
            early.append((shared[:, a, :], scales[:]))
        q00, q01 = early
        kb_col = keep.tile([P, PACK], F32, name="kb_col", tag="raw0a", align_bytes=LINE)
        nc.scalar.copy(kb_col[:], turned[1][:, :, LIVE])
        pairs = [
            [psum.tile([P, 2, CHUNK], F32, name="pair%d_%d" % (a, i), tag="bank%d" % (2 * a + i)) for i in range(2)]
            for a in range(2)
        ]

        def pair_passes(a, o, q):
            for r in range(PACK):
                one_pass(pairs[a][r // 2][:, r % 2, :], r, o, q, o == 0 and r % 2 == 0, o == 1 and r % 2 == 1)

        def pair_weights(a):
            for r in range(PACK):
                weigh(y[0][:, r, CHUNK * a : CHUNK * (a + 1)], pairs[a][r // 2][:, r % 2, :], r)
                if a == 1 and r % 2 == 1:
                    store_rows(0, r - 1)

        pair_passes(0, 0, q00)
        pair_passes(1, 0, q01)
        g10 = rounded(cols(raw1a, 0), nc.vector.tensor_copy, "g10", tag="kb_pool")
        g11 = keep.tile([P, CHUNK, PACK], BF16, name="g11", align_bytes=LINE)
        interleave(nc.scalar.copy, g11[:, 0 : PIECE - CHUNK, :], raw1a[:, :, CHUNK:PIECE])
        pair_passes(0, 1, quantize_q("q10", g10))
        pair_weights(0)
        interleave(nc.vector.tensor_copy, g11[:, PIECE - CHUNK : CHUNK, :], raw1b[:, :, 0 : HALF - PIECE])
        g12 = rounded(raw1b[:, :, HALF - PIECE : PIECE], nc.vector.tensor_copy, "g12", tag="g12")
        pair_passes(1, 1, quantize_q("q11", g11[:]))
        q12 = quantize_q("q12", g12)
        pair_weights(1)

        alone = [psum.tile([P, CHUNK], F32, name="alone%d" % r, tag="bank%d" % (4 + r)) for r in range(2)]
        pair = psum.tile([P, 2, CHUNK], F32, name="pair", tag="bank6")
        third = [alone[0][:], alone[1][:], pair[:, 0, :], pair[:, 1, :]]
        single = [psum.tile([P, CHUNK], F32, name="single%d" % r, tag="bank%d" % ((7 + r) % 8)) for r in range(PACK)]
        for r in range(PACK):
            one_pass(third[r], r, 1, q12, r != 3, False)
        g0b = keep.tile([P, HALF, PACK], BF16, name="g0b", tag="g12", align_bytes=LINE)
        g02, g03 = g0b[:, 0:CHUNK, :], g0b[:, CHUNK:HALF, :]
        interleave(nc.vector.tensor_copy, g02, cols(raw0b, 0))
        interleave(nc.vector.tensor_copy, g03, cols(raw0b, 1))
        q02 = quantize_q("q02", g02)
        q03 = quantize_q("q03", g03)
        for r in range(PACK):
            one_pass(third[r], r, 0, q02, False, r != 2)
        for r in range(PACK):
            one_pass(single[r][:], r, 0, q03, True, False)
        q13 = quantize_q("q13", rounded(raw13[:], nc.vector.tensor_copy, "g13"))
        yg0 = rounded(y[0][:], nc.vector.tensor_copy, "yg0", pool=relay, offset=5 * chunk_bytes)
        for r in range(PACK):
            one_pass(single[r][:], r, 1, q13, False, True)
        for r in range(PACK):
            weigh(y[1][:, r, 0:CHUNK], third[r], r)
        quantize_y(0, 2, yg0)
        for r in range(PACK):
            weigh(y[1][:, r, CHUNK:HALF], single[r][:], r)
            if r % 2 == 1:
                store_rows(1, r - 1)
        quantize_y(2, 1, rounded(y[1][:, :, 0:CHUNK], nc.vector.tensor_copy, "yg2"))
        nc.sync.dma_start(y_words[:, 0 : 3 * CHUNK], y_code[:, 0 : 3 * CHUNK].bitcast(I32))
        grouped = keep.tile([P, CHUNK, PACK], BF16, name="yg3", align_bytes=LINE)
        interleave(nc.vector.tensor_copy, grouped[:, 0:LAST, :], y[1][:, :, CHUNK : CHUNK + LAST])
        interleave(nc.scalar.copy, grouped[:, LAST:CHUNK, :], y[1][:, :, CHUNK + LAST : HALF])
        quantize_y(3, 1, grouped[:])
        nc.sync.dma_start(y_words[:, 3 * CHUNK : NQ], y_code[:, 3 * CHUNK : NQ].bitcast(I32))
        for quad in range(4):
            queue = nc.scalar if quad < 2 else nc.sync
            queue.dma_start(
                out_2[0, 4 * quad : 4 * quad + 4, :].bitcast(I32),
                y_scale[32 * quad : 32 * quad + 4, :].bitcast(I32),
            )
